import numpy as np
import ml_dtypes


def mxq(x, axis, fmt="e4m3"):
    dtype, down = {"e4m3": (ml_dtypes.float8_e4m3fn, 7), "e5m2": (ml_dtypes.float8_e5m2, 14)}[fmt]
    v = np.moveaxis(np.asarray(x, np.float32).astype(ml_dtypes.bfloat16).astype(np.float64), axis, -1)
    blocks = v.reshape(v.shape[:-1] + (-1, 32))
    amax = np.abs(blocks).max(-1, keepdims=True)
    byte = np.maximum(np.where(amax > 0, np.frexp(amax)[1] - 1 + 127, 0) - down, 1)
    scale = np.exp2(byte - 127.0)
    codes = (blocks / scale).astype(np.float32).astype(dtype).astype(np.float64)
    return np.moveaxis((codes * scale).reshape(v.shape), -1, axis)


WIDE = False


def mx_kscale(k):
    if not WIDE:
        return np.ones(k)
    levels = np.array([10, -10, 5, -5, 0])
    if k % 512:
        return np.exp2(np.random.permutation(np.resize(levels, k // 32))).repeat(32)
    a = np.empty((k // 512, 16))
    for p in range(k // 512):
        a[p, :8] = np.random.permutation(np.resize(levels, 8))
        for g in range(8):
            far = levels[np.abs(levels - a[p, g]) >= 10]
            a[p, g + 8] = far[np.random.randint(len(far))]
    return np.exp2(a.ravel()).repeat(32)


def f64(x):
    return np.asarray(x).astype(np.float64)


def striped(idx):
    return np.tile(np.asarray(idx).reshape(-1, 16).T, (8, 1)).astype(np.uint16)


def unstriped(offs):
    return offs[:16].T.reshape(-1).astype(np.int64)


def bf(x):
    return np.asarray(x, np.float32).astype(ml_dtypes.bfloat16)


def planes(Y):
    r, m = Y.shape
    b = f64(bf(Y)).reshape(r // 32, 32, m)
    amax = np.abs(b).max(1)
    byte = np.clip(np.where(amax > 0, np.frexp(amax)[1] - 1 + 127 - 7, 1), 1, 254)
    codes = (b * np.exp2(127.0 - byte)[:, None, :]).reshape(r, m).astype(np.float32).astype(ml_dtypes.float8_e4m3fn).view(np.uint8)
    words = codes.reshape(r // 512, 128, 4, m).transpose(0, 1, 3, 2)
    return np.ascontiguousarray(words), np.ascontiguousarray(byte.astype(np.uint8).reshape(r // 512, 16, m))


R, K, T, I, G, F = 512, 512, 2048, 1024, 128, 512


def setup_inputs():
    n = np.random.standard_normal
    idx = np.random.permutation(T)[:I]
    fr = mx_kscale(R)
    fk = mx_kscale(K)
    return {
        "rad": (np.exp(-np.square(n((R, I)))) * fr[:, None]).astype(np.float32),
        "wr": (n((R, K)) * 1.5 / np.sqrt(R) / fr[:, None]).astype(np.float32),
        "atom": (n((K, T)) / fk[:, None]).astype(np.float32),
        "wo": (n((K, F)) * 0.4 / np.sqrt(K) * fk[:, None]).astype(np.float32),
        "offs": striped(idx),
    }


def reference(rad, wr, atom, wo, offs):
    idx = unstriped(offs)
    wrq = mxq(f64(wr), 0, "e4m3")
    radq = mxq(f64(rad), 0, "e4m3")
    z = wrq.T @ radq
    x = f64(atom)[:, idx] * z
    b = x.reshape(K, G, I // G).sum(axis=2)
    woq = mxq(f64(wo), 0, "e4m3")
    bq = mxq(b, 0, "e4m3")
    y = woq.T @ bq
    words, scales = planes(y)
    return y, words, scales

@@ -1,0 +1,172 @@
+from contextlib import ExitStack
+
+import concourse.mybir as mybir
+from concourse.masks import make_identity
+
+R, K, T, I, G, F = 512, 512, 2048, 1024, 128, 512
+FLOPS = 2 * R * K * I + 2 * K * F * G
+
+F32 = mybir.dt.float32
+BF16 = mybir.dt.bfloat16
+I32 = mybir.dt.int32
+U32 = mybir.dt.uint32
+U16 = mybir.dt.uint16
+U8 = mybir.dt.uint8
+FP8X4 = mybir.dt.float8_e4m3fn_x4
+MULT = mybir.AluOpType.mult
+ADD = mybir.AluOpType.add
+
+P = 128
+PACK = 4
+EDGES = I // G
+HALF = I // 2
+WR_SPLIT = 88
+RAD_SPLIT = 344
+
+
+def tile_attend_filterconv_pl_kernel(tc, rad, wr, atom, wo, offs, out_0, out_1, out_2):
+    nc = tc.nc
+    with ExitStack() as ctx:
+        sb = ctx.enter_context(tc.tile_pool(name="sb", bufs=1))
+        ps = ctx.enter_context(tc.psum_pool(name="ps", bufs=1))
+
+        offsets = sb.tile([P, I // 16], U16, name="offsets")
+        nc.sync.dma_start(offsets[:], offs)
+
+        wr_raw = sb.tile([P, PACK, K], F32, name="wr_raw")
+        nc.sync.dma_start(wr_raw[:], wr.rearrange("(p j) k -> p j k", j=PACK))
+        rad_rows = rad.rearrange("(p j) i -> p j i", j=PACK)
+        rad_raw = []
+        for h in range(2):
+            raw = sb.tile([P, PACK, HALF], F32, name="rad_raw%d" % h)
+            nc.sync.dma_start(raw[:], rad_rows[:, :, h * HALF : (h + 1) * HALF])
+            rad_raw.append(raw)
+        atom_rows = atom.rearrange("(p t) n -> p t n", t=PACK)
+        atoms = []
+        for t in range(PACK):
+            a = sb.tile([P, T], F32, name="atom%d" % t)
+            nc.sync.dma_start(a[:], atom_rows[:, t, :])
+            atoms.append(a)
+        wo_rows = wo.rearrange("(p j) f -> p j f", j=PACK)
+        wo_raw = []
+        for h in range(2):
+            raw = sb.tile([P, PACK, F // 2], F32, name="wo_raw%d" % h)
+            nc.sync.dma_start(raw[:], wo_rows[:, :, h * (F // 2) : (h + 1) * (F // 2)])
+            wo_raw.append(raw)
+
+        ident = sb.tile([P, P], F32, name="ident")
+        make_identity(nc, ident[:])
+
+        wr_bf = sb.tile([P, K * PACK], BF16, name="wr_bf", align_bytes=64)
+        wr_dst = wr_bf[:].rearrange("p (t m j) -> p m j t", t=PACK, j=PACK)
+        wr_src = wr_raw[:].rearrange("p j (m t) -> p m j t", t=PACK)
+        nc.vector.tensor_copy(wr_dst[:, :WR_SPLIT, :, :], wr_src[:, :WR_SPLIT, :, :])
+        nc.scalar.copy(wr_dst[:, WR_SPLIT:, :, :], wr_src[:, WR_SPLIT:, :, :])
+        wr_codes = sb.tile([P, K], U32, name="wr_codes", align_bytes=64)
+        wr_scales = sb.tile([P, K], U8, name="wr_scales", align_bytes=64)
+        nc.vector.quantize_mx(out=wr_codes[:].bitcast(FP8X4), scales=wr_scales[:], in_=wr_bf[:])
+
+        z = [sb.tile([P, I], F32, name="z%d" % t) for t in range(PACK)]
+        for h in range(2):
+            rad_bf = sb.tile([P, HALF * PACK], BF16, name="rad_bf%d" % h, align_bytes=64)
+            dst = rad_bf[:].rearrange("p (c i j) -> p c j i", i=4, j=PACK)
+            src = rad_raw[h][:].rearrange("p j (c i) -> p c j i", i=4)
+            if h == 0:
+                nc.vector.tensor_copy(dst[:, : RAD_SPLIT // 4, :, :], src[:, : RAD_SPLIT // 4, :, :])
+                nc.scalar.copy(dst[:, RAD_SPLIT // 4 :, :, :], src[:, RAD_SPLIT // 4 :, :, :])
+            else:
+                nc.vector.tensor_copy(dst, src)
+            rad_codes = sb.tile([P, HALF], U32, name="rad_codes%d" % h, align_bytes=64)
+            rad_scales = sb.tile([P, HALF], U8, name="rad_scales%d" % h, align_bytes=64)
+            nc.vector.quantize_mx(out=rad_codes[:].bitcast(FP8X4), scales=rad_scales[:], in_=rad_bf[:])
+            for t in range(PACK):
+                bank = ps.tile([P, HALF], F32, name="mm", tag="mm", bufs=4)
+                cols = slice(t * P, (t + 1) * P)
+                nc.tensor.matmul_mx(
+                    out=bank[:],
+                    lhsT=wr_codes[:, cols].bitcast(FP8X4),
+                    lhsT_scale=wr_scales[:, cols],
+                    rhs=rad_codes[:].bitcast(FP8X4),
+                    rhs_scale=rad_scales[:],
+                    start=True,
+                    stop=True,
+                )
+                nc.scalar.copy(z[t][:, h * HALF : (h + 1) * HALF], bank[:])
+
+        b_bf = sb.tile([P, G, PACK], BF16, name="b_bf", align_bytes=64)
+        b_back = ps.tile([P, PACK - 1, G], F32, name="b_back")
+        wo_bf = sb.tile([P, F * PACK], BF16, name="wo_bf", align_bytes=64)
+        wo_dst = wo_bf[:].rearrange("p (t m j) -> p m j t", t=PACK, j=PACK)
+        for t in range(PACK):
+            x = sb.tile([P, I], F32, name="x%d" % t)
+            if t == 0:
+                for h in range(2):
+                    nc.vector.tensor_tensor(
+                        x[:, h * HALF : (h + 1) * HALF],
+                        atoms[t][:].indirect(offsets[:, h * (HALF // 16) : (h + 1) * (HALF // 16)]),
+                        z[t][:, h * HALF : (h + 1) * HALF],
+                        MULT,
+                    )
+            else:
+                nc.vector.tensor_tensor(x[:], atoms[t][:].indirect(offsets[:]), z[t][:], MULT)
+            if t == PACK - 1:
+                with nc.allow_low_precision(reason="float32 sum, rounded once to bfloat16 for the quantiser"):
+                    nc.vector.tensor_reduce(
+                        out=b_bf[:, :, t],
+                        in_=x[:].rearrange("p (g e) -> p g e", e=EDGES),
+                        axis=mybir.AxisListType.X,
+                        op=ADD,
+                    )
+                continue
+            if t == PACK - 2:
+                nc.scalar.copy(wo_dst[:, : P // 2, :, :], wo_raw[0][:].rearrange("p j (m t) -> p m j t", t=PACK))
+            sums = ps.tile([P, P], F32, name="sums", tag="sums", bufs=2)
+            for e in range(EDGES):
+                nc.tensor.matmul(
+                    sums[:], x[:, e:I:EDGES], ident[:], start=(e == 0), stop=(e == EDGES - 1), is_transpose=True
+                )
+            sums_sb = sb.tile([P, P], F32, name="sums_sb%d" % t)
+            nc.scalar.copy(sums_sb[:], sums[:])
+            nc.tensor.transpose(b_back[:, t, :], sums_sb[:], ident[:])
+            if t == 1:
+                nc.scalar.copy(b_bf[:, :, 0:2], b_back[:, 0:2, :].rearrange("p t g -> p g t"))
+        nc.scalar.copy(wo_dst[:, P // 2 :, :, :], wo_raw[1][:].rearrange("p j (m t) -> p m j t", t=PACK))
+        nc.vector.tensor_copy(b_bf[:, :, 2], b_back[:, 2, :])
+
+        b_codes = sb.tile([P, G], U32, name="b_codes", align_bytes=64)
+        b_scales = sb.tile([P, G], U8, name="b_scales", align_bytes=64)
+        nc.vector.quantize_mx(
+            out=b_codes[:].bitcast(FP8X4), scales=b_scales[:], in_=b_bf[:].rearrange("p g t -> p (g t)")
+        )
+        y = sb.tile([P, PACK, G], F32, name="y")
+        for t in range(PACK):
+            wo_codes = sb.tile([P, P], U32, name="wo_codes%d" % t, align_bytes=64)
+            wo_scales = sb.tile([P, P], U8, name="wo_scales%d" % t, align_bytes=64)
+            nc.vector.quantize_mx(
+                out=wo_codes[:].bitcast(FP8X4), scales=wo_scales[:], in_=wo_bf[:, t * P * PACK : (t + 1) * P * PACK]
+            )
+            bank = ps.tile([P, HALF], F32, name="mm", tag="mm", bufs=4)
+            nc.tensor.matmul_mx(
+                out=bank[:, :G],
+                lhsT=wo_codes[:].bitcast(FP8X4),
+                lhsT_scale=wo_scales[:],
+                rhs=b_codes[:].bitcast(FP8X4),
+                rhs_scale=b_scales[:],
+                start=True,
+                stop=True,
+            )
+            nc.scalar.copy(y[:, t, :], bank[:, :G])
+        nc.sync.dma_start(out_0.rearrange("(p t) g -> p t g", t=PACK), y[:])
+
+        y_bf = sb.tile([P, G * PACK], BF16, name="y_bf", align_bytes=64)
+        nc.vector.tensor_copy(
+            y_bf[:].rearrange("p (c i t) -> p c t i", i=4, t=PACK), y[:].rearrange("p t (c i) -> p c t i", i=4)
+        )
+        y_codes = sb.tile([P, G], U32, name="y_codes", align_bytes=64)
+        y_scales = sb.tile([P, G], U8, name="y_scales", align_bytes=64)
+        nc.vector.quantize_mx(out=y_codes[:].bitcast(FP8X4), scales=y_scales[:], in_=y_bf[:])
+        nc.sync.dma_start(out_1[0].rearrange("l c r -> l (c r)").bitcast(I32), y_codes[:].bitcast(I32))
+        scale_rows = out_2[0].bitcast(I32)
+        for q in range(4):
+            queue = nc.scalar if q % 2 == 0 else nc.sync
+            queue.dma_start(scale_rows[4 * q : 4 * q + 4, :], y_scales[32 * q : 32 * q + 4, :].bitcast(I32))

@@ -22,6 +22,8 @@ EDGES = I // G
 HALF = I // 2
 WR_SPLIT = 88
 RAD_SPLIT = 344
+WO_CUTS = (0, 32, 80, 128)
+ORDER = (2, 0, 1, 3)
 
 
 def tile_attend_filterconv_pl_kernel(tc, rad, wr, atom, wo, offs, out_0, out_1, out_2):
@@ -31,28 +33,32 @@ def tile_attend_filterconv_pl_kernel(tc, rad, wr, atom, wo, offs, out_0, out_1, 
         ps = ctx.enter_context(tc.psum_pool(name="ps", bufs=1))
 
         offsets = sb.tile([P, I // 16], U16, name="offsets")
-        nc.sync.dma_start(offsets[:], offs)
 
         wr_raw = sb.tile([P, PACK, K], F32, name="wr_raw")
         nc.sync.dma_start(wr_raw[:], wr.rearrange("(p j) k -> p j k", j=PACK))
         rad_rows = rad.rearrange("(p j) i -> p j i", j=PACK)
         rad_raw = []
         for h in range(2):
-            raw = sb.tile([P, PACK, HALF], F32, name="rad_raw%d" % h)
+            raw = sb.tile([P, PACK, HALF], F32, name="rad_raw%d" % h, tag="rad_raw%d" % h)
             nc.sync.dma_start(raw[:], rad_rows[:, :, h * HALF : (h + 1) * HALF])
             rad_raw.append(raw)
+        nc.sync.dma_start(offsets[:], offs)
         atom_rows = atom.rearrange("(p t) n -> p t n", t=PACK)
-        atoms = []
-        for t in range(PACK):
-            a = sb.tile([P, T], F32, name="atom%d" % t)
-            nc.sync.dma_start(a[:], atom_rows[:, t, :])
-            atoms.append(a)
         wo_rows = wo.rearrange("(p j) f -> p j f", j=PACK)
-        wo_raw = []
-        for h in range(2):
-            raw = sb.tile([P, PACK, F // 2], F32, name="wo_raw%d" % h)
-            nc.sync.dma_start(raw[:], wo_rows[:, :, h * (F // 2) : (h + 1) * (F // 2)])
-            wo_raw.append(raw)
+        atoms = [sb.tile([P, T], F32, name="atom%d" % t) for t in range(PACK)]
+        wo_raw = [
+            sb.tile([P, PACK, PACK * (WO_CUTS[n + 1] - WO_CUTS[n])], F32, name="wo_raw%d" % n) for n in range(3)
+        ]
+
+        def load_wo(n):
+            nc.sync.dma_start(wo_raw[n][:], wo_rows[:, :, PACK * WO_CUTS[n] : PACK * WO_CUTS[n + 1]])
+
+        for t in ORDER[:-1]:
+            nc.sync.dma_start(atoms[t][:], atom_rows[:, t, :])
+        load_wo(0)
+        nc.sync.dma_start(atoms[PACK - 1][:], atom_rows[:, PACK - 1, :])
+        load_wo(1)
+        load_wo(2)
 
         ident = sb.tile([P, P], F32, name="ident")
         make_identity(nc, ident[:])
@@ -66,40 +72,60 @@ def tile_attend_filterconv_pl_kernel(tc, rad, wr, atom, wo, offs, out_0, out_1, 
         wr_scales = sb.tile([P, K], U8, name="wr_scales", align_bytes=64)
         nc.vector.quantize_mx(out=wr_codes[:].bitcast(FP8X4), scales=wr_scales[:], in_=wr_bf[:])
 
-        z = [sb.tile([P, I], F32, name="z%d" % t) for t in range(PACK)]
-        for h in range(2):
-            rad_bf = sb.tile([P, HALF * PACK], BF16, name="rad_bf%d" % h, align_bytes=64)
+        z = [
+            sb.tile([P, I], F32, name="z%d" % t, tag="rad_raw1" if t == ORDER[0] else "z%d" % t) for t in range(PACK)
+        ]
+        rad_codes, rad_scales = [], []
+
+        def quantise_rad(h):
+            rad_bf = sb.tile([P, HALF * PACK], BF16, name="rad_bf%d" % h, tag="rad_bf%d" % h, align_bytes=64)
             dst = rad_bf[:].rearrange("p (c i j) -> p c j i", i=4, j=PACK)
             src = rad_raw[h][:].rearrange("p j (c i) -> p c j i", i=4)
-            if h == 0:
-                nc.vector.tensor_copy(dst[:, : RAD_SPLIT // 4, :, :], src[:, : RAD_SPLIT // 4, :, :])
-                nc.scalar.copy(dst[:, RAD_SPLIT // 4 :, :, :], src[:, RAD_SPLIT // 4 :, :, :])
-            else:
-                nc.vector.tensor_copy(dst, src)
-            rad_codes = sb.tile([P, HALF], U32, name="rad_codes%d" % h, align_bytes=64)
-            rad_scales = sb.tile([P, HALF], U8, name="rad_scales%d" % h, align_bytes=64)
-            nc.vector.quantize_mx(out=rad_codes[:].bitcast(FP8X4), scales=rad_scales[:], in_=rad_bf[:])
-            for t in range(PACK):
-                bank = ps.tile([P, HALF], F32, name="mm", tag="mm", bufs=4)
-                cols = slice(t * P, (t + 1) * P)
-                nc.tensor.matmul_mx(
-                    out=bank[:],
-                    lhsT=wr_codes[:, cols].bitcast(FP8X4),
-                    lhsT_scale=wr_scales[:, cols],
-                    rhs=rad_codes[:].bitcast(FP8X4),
-                    rhs_scale=rad_scales[:],
-                    start=True,
-                    stop=True,
-                )
-                nc.scalar.copy(z[t][:, h * HALF : (h + 1) * HALF], bank[:])
+            nc.vector.tensor_copy(dst[:, : RAD_SPLIT // 4, :, :], src[:, : RAD_SPLIT // 4, :, :])
+            nc.scalar.copy(dst[:, RAD_SPLIT // 4 :, :, :], src[:, RAD_SPLIT // 4 :, :, :])
+            codes = sb.tile([P, HALF], U32, name="rad_codes%d" % h, align_bytes=64)
+            scales = sb.tile([P, HALF], U8, name="rad_scales%d" % h, align_bytes=64)
+            nc.vector.quantize_mx(out=codes[:].bitcast(FP8X4), scales=scales[:], in_=rad_bf[:])
+            rad_codes.append(codes)
+            rad_scales.append(scales)
 
-        b_bf = sb.tile([P, G, PACK], BF16, name="b_bf", align_bytes=64)
-        b_back = ps.tile([P, PACK - 1, G], F32, name="b_back")
+        def filters(t, h):
+            bank = ps.tile([P, HALF], F32, name="mm", tag="mm", bufs=3)
+            cols = slice(t * P, (t + 1) * P)
+            nc.tensor.matmul_mx(
+                out=bank[:],
+                lhsT=wr_codes[:, cols].bitcast(FP8X4),
+                lhsT_scale=wr_scales[:, cols],
+                rhs=rad_codes[h][:].bitcast(FP8X4),
+                rhs_scale=rad_scales[h][:],
+                start=True,
+                stop=True,
+            )
+            nc.scalar.copy(z[t][:, h * HALF : (h + 1) * HALF], bank[:])
+
+        quantise_rad(0)
+        quantise_rad(1)
+        for t in ORDER:
+            for h in range(2):
+                filters(t, h)
+
+        b_bf = sb.tile([P, G, PACK], BF16, name="b_bf", tag="b_bf", align_bytes=64)
         wo_bf = sb.tile([P, F * PACK], BF16, name="wo_bf", align_bytes=64)
         wo_dst = wo_bf[:].rearrange("p (t m j) -> p m j t", t=PACK, j=PACK)
-        for t in range(PACK):
-            x = sb.tile([P, I], F32, name="x%d" % t)
-            if t == 0:
+
+        def cast_wo(n):
+            nc.scalar.copy(
+                wo_dst[:, WO_CUTS[n] : WO_CUTS[n + 1], :, :], wo_raw[n][:].rearrange("p j (m t) -> p m j t", t=PACK)
+            )
+
+        sums_first = sb.tile([P, P], F32, name="sums_first")
+        sums_sb = [sums_first[:], wo_raw[0][:, 0, :P], wo_raw[2][:, 0, :P]]
+        back_first = ps.tile([P, G], F32, name="back_first")
+        back_pair = ps.tile([P, 2, G], F32, name="back_pair")
+        backs = [back_first[:], back_pair[:, 0, :], back_pair[:, 1, :]]
+        for n, t in enumerate(ORDER):
+            x = sb.tile([P, I], F32, name="x%d" % t, tag="rad_bf1" if n == 0 else "x%d" % t, align_bytes=64)
+            if n == 0:
                 for h in range(2):
                     nc.vector.tensor_tensor(
                         x[:, h * HALF : (h + 1) * HALF],
@@ -109,7 +135,7 @@ def tile_attend_filterconv_pl_kernel(tc, rad, wr, atom, wo, offs, out_0, out_1, 
                     )
             else:
                 nc.vector.tensor_tensor(x[:], atoms[t][:].indirect(offsets[:]), z[t][:], MULT)
-            if t == PACK - 1:
+            if n == PACK - 1:
                 with nc.allow_low_precision(reason="float32 sum, rounded once to bfloat16 for the quantiser"):
                     nc.vector.tensor_reduce(
                         out=b_bf[:, :, t],
@@ -118,38 +144,50 @@ def tile_attend_filterconv_pl_kernel(tc, rad, wr, atom, wo, offs, out_0, out_1, 
                         op=ADD,
                     )
                 continue
-            if t == PACK - 2:
-                nc.scalar.copy(wo_dst[:, : P // 2, :, :], wo_raw[0][:].rearrange("p j (m t) -> p m j t", t=PACK))
+            if n == 1:
+                cast_wo(0)
+            if n == 2:
+                cast_wo(1)
+                cast_wo(2)
             sums = ps.tile([P, P], F32, name="sums", tag="sums", bufs=2)
             for e in range(EDGES):
                 nc.tensor.matmul(
                     sums[:], x[:, e:I:EDGES], ident[:], start=(e == 0), stop=(e == EDGES - 1), is_transpose=True
                 )
-            sums_sb = sb.tile([P, P], F32, name="sums_sb%d" % t)
-            nc.scalar.copy(sums_sb[:], sums[:])
-            nc.tensor.transpose(b_back[:, t, :], sums_sb[:], ident[:])
-            if t == 1:
-                nc.scalar.copy(b_bf[:, :, 0:2], b_back[:, 0:2, :].rearrange("p t g -> p g t"))
-        nc.scalar.copy(wo_dst[:, P // 2 :, :, :], wo_raw[1][:].rearrange("p j (m t) -> p m j t", t=PACK))
-        nc.vector.tensor_copy(b_bf[:, :, 2], b_back[:, 2, :])
+            nc.scalar.copy(sums_sb[n], sums[:])
+            nc.tensor.transpose(backs[n], sums_sb[n], ident[:])
+            if n == 0:
+                nc.scalar.copy(b_bf[:, :, 2:4], back_first[:].unsqueeze(2).to_broadcast([P, G, 2]))
+            if n == 2:
+                nc.scalar.copy(b_bf[:, :, 0:2], back_pair[:].rearrange("p t g -> p g t"))
 
+        def quantise_wo(u, tag):
+            codes = sb.tile([P, 2 * P], U32, name="wo_codes%d" % u, align_bytes=64)
+            scales = sb.tile([P, 2 * P], U8, name="wo_scales%d" % u, tag=tag, align_bytes=64)
+            nc.vector.quantize_mx(
+                out=codes[:].bitcast(FP8X4), scales=scales[:], in_=wo_bf[:, u * 2 * P * PACK : (u + 1) * 2 * P * PACK]
+            )
+            return codes, scales
+
+        wo_q = [quantise_wo(0, "wo_scales0")]
         b_codes = sb.tile([P, G], U32, name="b_codes", align_bytes=64)
         b_scales = sb.tile([P, G], U8, name="b_scales", align_bytes=64)
         nc.vector.quantize_mx(
             out=b_codes[:].bitcast(FP8X4), scales=b_scales[:], in_=b_bf[:].rearrange("p g t -> p (g t)")
         )
+        wo_q.append(quantise_wo(1, "b_bf"))
         y = sb.tile([P, PACK, G], F32, name="y")
         for t in range(PACK):
-            wo_codes = sb.tile([P, P], U32, name="wo_codes%d" % t, align_bytes=64)
-            wo_scales = sb.tile([P, P], U8, name="wo_scales%d" % t, align_bytes=64)
-            nc.vector.quantize_mx(
-                out=wo_codes[:].bitcast(FP8X4), scales=wo_scales[:], in_=wo_bf[:, t * P * PACK : (t + 1) * P * PACK]
-            )
-            bank = ps.tile([P, HALF], F32, name="mm", tag="mm", bufs=4)
+            codes, scales = wo_q[t // 2]
+            cols = slice((t % 2) * P, (t % 2 + 1) * P)
+            if t < 3:
+                bank = ps.tile([P, HALF], F32, name="mm", tag="mm", bufs=3)
+            else:
+                bank = ps.tile([P, HALF], F32, name="mm_last")
             nc.tensor.matmul_mx(
                 out=bank[:, :G],
-                lhsT=wo_codes[:].bitcast(FP8X4),
-                lhsT_scale=wo_scales[:],
+                lhsT=codes[:, cols].bitcast(FP8X4),
+                lhsT_scale=scales[:, cols],
                 rhs=b_codes[:].bitcast(FP8X4),
                 rhs_scale=b_scales[:],
                 start=True,

@@ -22,7 +22,7 @@ EDGES = I // G
 HALF = I // 2
 WR_SPLIT = 88
 RAD_SPLIT = 344
-WO_CUTS = (0, 32, 80, 128)
+WO_CUTS = (0, 64, 128)
 ORDER = (2, 0, 1, 3)
 
 
@@ -47,7 +47,7 @@ def tile_attend_filterconv_pl_kernel(tc, rad, wr, atom, wo, offs, out_0, out_1, 
         wo_rows = wo.rearrange("(p j) f -> p j f", j=PACK)
         atoms = [sb.tile([P, T], F32, name="atom%d" % t) for t in range(PACK)]
         wo_raw = [
-            sb.tile([P, PACK, PACK * (WO_CUTS[n + 1] - WO_CUTS[n])], F32, name="wo_raw%d" % n) for n in range(3)
+            sb.tile([P, PACK, PACK * (WO_CUTS[n + 1] - WO_CUTS[n])], F32, name="wo_raw%d" % n) for n in range(2)
         ]
 
         def load_wo(n):
@@ -55,17 +55,16 @@ def tile_attend_filterconv_pl_kernel(tc, rad, wr, atom, wo, offs, out_0, out_1, 
 
         for t in ORDER[:-1]:
             nc.sync.dma_start(atoms[t][:], atom_rows[:, t, :])
-        load_wo(0)
         nc.sync.dma_start(atoms[PACK - 1][:], atom_rows[:, PACK - 1, :])
+        load_wo(0)
         load_wo(1)
-        load_wo(2)
 
         ident = sb.tile([P, P], F32, name="ident")
         make_identity(nc, ident[:])
 
         wr_bf = sb.tile([P, K * PACK], BF16, name="wr_bf", align_bytes=64)
-        wr_dst = wr_bf[:].rearrange("p (t m j) -> p m j t", t=PACK, j=PACK)
-        wr_src = wr_raw[:].rearrange("p j (m t) -> p m j t", t=PACK)
+        wr_dst = wr_bf[:].rearrange("p (t m j) -> p m t j", t=PACK, j=PACK)
+        wr_src = wr_raw[:].rearrange("p j (m t) -> p m t j", t=PACK)
         nc.vector.tensor_copy(wr_dst[:, :WR_SPLIT, :, :], wr_src[:, :WR_SPLIT, :, :])
         nc.scalar.copy(wr_dst[:, WR_SPLIT:, :, :], wr_src[:, WR_SPLIT:, :, :])
         wr_codes = sb.tile([P, K], U32, name="wr_codes", align_bytes=64)
@@ -111,21 +110,22 @@ def tile_attend_filterconv_pl_kernel(tc, rad, wr, atom, wo, offs, out_0, out_1, 
 
         b_bf = sb.tile([P, G, PACK], BF16, name="b_bf", tag="b_bf", align_bytes=64)
         wo_bf = sb.tile([P, F * PACK], BF16, name="wo_bf", align_bytes=64)
-        wo_dst = wo_bf[:].rearrange("p (t m j) -> p m j t", t=PACK, j=PACK)
+        wo_dst = wo_bf[:].rearrange("p (t m j) -> p m t j", t=PACK, j=PACK)
 
         def cast_wo(n):
             nc.scalar.copy(
-                wo_dst[:, WO_CUTS[n] : WO_CUTS[n + 1], :, :], wo_raw[n][:].rearrange("p j (m t) -> p m j t", t=PACK)
+                wo_dst[:, WO_CUTS[n] : WO_CUTS[n + 1], :, :], wo_raw[n][:].rearrange("p j (m t) -> p m t j", t=PACK)
             )
 
         sums_first = sb.tile([P, P], F32, name="sums_first")
-        sums_sb = [sums_first[:], wo_raw[0][:, 0, :P], wo_raw[2][:, 0, :P]]
+        sums_second = sb.tile([P, P], F32, name="sums_second")
+        sums_sb = [sums_first[:], sums_second[:], wo_raw[0][:, 0, :P]]
         back_first = ps.tile([P, G], F32, name="back_first")
         back_pair = ps.tile([P, 2, G], F32, name="back_pair")
         backs = [back_first[:], back_pair[:, 0, :], back_pair[:, 1, :]]
         for n, t in enumerate(ORDER):
             x = sb.tile([P, I], F32, name="x%d" % t, tag="rad_bf1" if n == 0 else "x%d" % t, align_bytes=64)
-            if n == 0:
+            if n in (0, PACK - 1):
                 for h in range(2):
                     nc.vector.tensor_tensor(
                         x[:, h * HALF : (h + 1) * HALF],
@@ -137,18 +137,17 @@ def tile_attend_filterconv_pl_kernel(tc, rad, wr, atom, wo, offs, out_0, out_1, 
                 nc.vector.tensor_tensor(x[:], atoms[t][:].indirect(offsets[:]), z[t][:], MULT)
             if n == PACK - 1:
                 with nc.allow_low_precision(reason="float32 sum, rounded once to bfloat16 for the quantiser"):
-                    nc.vector.tensor_reduce(
-                        out=b_bf[:, :, t],
-                        in_=x[:].rearrange("p (g e) -> p g e", e=EDGES),
-                        axis=mybir.AxisListType.X,
-                        op=ADD,
-                    )
+                    for h in range(2):
+                        nc.vector.tensor_reduce(
+                            out=b_bf[:, h * (G // 2) : (h + 1) * (G // 2), t],
+                            in_=x[:, h * HALF : (h + 1) * HALF].rearrange("p (g e) -> p g e", e=EDGES),
+                            axis=mybir.AxisListType.X,
+                            op=ADD,
+                        )
+                nc.vector.tensor_copy(b_bf[:, :, 0:2], back_pair[:].rearrange("p t g -> p g t"))
                 continue
-            if n == 1:
-                cast_wo(0)
             if n == 2:
-                cast_wo(1)
-                cast_wo(2)
+                cast_wo(0)
             sums = ps.tile([P, P], F32, name="sums", tag="sums", bufs=2)
             for e in range(EDGES):
                 nc.tensor.matmul(
@@ -159,7 +158,7 @@ def tile_attend_filterconv_pl_kernel(tc, rad, wr, atom, wo, offs, out_0, out_1, 
             if n == 0:
                 nc.scalar.copy(b_bf[:, :, 2:4], back_first[:].unsqueeze(2).to_broadcast([P, G, 2]))
             if n == 2:
-                nc.scalar.copy(b_bf[:, :, 0:2], back_pair[:].rearrange("p t g -> p g t"))
+                cast_wo(1)
 
         def quantise_wo(u, tag):
             codes = sb.tile([P, 2 * P], U32, name="wo_codes%d" % u, align_bytes=64)

@@ -144,7 +144,6 @@ def tile_attend_filterconv_pl_kernel(tc, rad, wr, atom, wo, offs, out_0, out_1, 
                             axis=mybir.AxisListType.X,
                             op=ADD,
                         )
-                nc.vector.tensor_copy(b_bf[:, :, 0:2], back_pair[:].rearrange("p t g -> p g t"))
                 continue
             if n == 2:
                 cast_wo(0)
@@ -159,6 +158,7 @@ def tile_attend_filterconv_pl_kernel(tc, rad, wr, atom, wo, offs, out_0, out_1, 
                 nc.scalar.copy(b_bf[:, :, 2:4], back_first[:].unsqueeze(2).to_broadcast([P, G, 2]))
             if n == 2:
                 cast_wo(1)
+                nc.scalar.copy(b_bf[:, :, 0:2], back_pair[:].rearrange("p t g -> p g t"))
 
         def quantise_wo(u, tag):
             codes = sb.tile([P, 2 * P], U32, name="wo_codes%d" % u, align_bytes=64)

@@ -46,12 +46,12 @@ def tile_attend_filterconv_pl_kernel(tc, rad, wr, atom, wo, offs, out_0, out_1, 
         atom_rows = atom.rearrange("(p t) n -> p t n", t=PACK)
         wo_rows = wo.rearrange("(p j) f -> p j f", j=PACK)
         atoms = [sb.tile([P, T], F32, name="atom%d" % t) for t in range(PACK)]
-        wo_raw = [
-            sb.tile([P, PACK, PACK * (WO_CUTS[n + 1] - WO_CUTS[n])], F32, name="wo_raw%d" % n) for n in range(2)
-        ]
+        wo_area = sb.tile([P, 2 * I], F32, name="wo_area", align_bytes=64)
+        wo_second = sb.tile([P, PACK, F // 2], F32, name="wo_second")
+        wo_raw = [wo_area[:, I:].rearrange("p (j f) -> p j f", j=PACK), wo_second[:]]
 
         def load_wo(n):
-            nc.sync.dma_start(wo_raw[n][:], wo_rows[:, :, PACK * WO_CUTS[n] : PACK * WO_CUTS[n + 1]])
+            nc.sync.dma_start(wo_raw[n], wo_rows[:, :, PACK * WO_CUTS[n] : PACK * WO_CUTS[n + 1]])
 
         for t in ORDER[:-1]:
             nc.sync.dma_start(atoms[t][:], atom_rows[:, t, :])
@@ -109,17 +109,16 @@ def tile_attend_filterconv_pl_kernel(tc, rad, wr, atom, wo, offs, out_0, out_1, 
                 filters(t, h)
 
         b_bf = sb.tile([P, G, PACK], BF16, name="b_bf", tag="b_bf", align_bytes=64)
-        wo_bf = sb.tile([P, F * PACK], BF16, name="wo_bf", align_bytes=64)
+        wo_bf = wo_area[:, :I].bitcast(BF16)
         wo_dst = wo_bf[:].rearrange("p (t m j) -> p m t j", t=PACK, j=PACK)
 
-        def cast_wo(n):
-            nc.scalar.copy(
-                wo_dst[:, WO_CUTS[n] : WO_CUTS[n + 1], :, :], wo_raw[n][:].rearrange("p j (m t) -> p m t j", t=PACK)
-            )
+        def cast_wo(n, tiles):
+            src = wo_raw[n].rearrange("p j (m t) -> p m t j", t=PACK)
+            nc.scalar.copy(wo_dst[:, WO_CUTS[n] : WO_CUTS[n + 1], tiles, :], src[:, :, tiles, :])
 
         sums_first = sb.tile([P, P], F32, name="sums_first")
         sums_second = sb.tile([P, P], F32, name="sums_second")
-        sums_sb = [sums_first[:], sums_second[:], wo_raw[0][:, 0, :P]]
+        sums_sb = [sums_first[:], sums_second[:], wo_area[:, I - P // 2 : I + P // 2]]
         back_first = ps.tile([P, G], F32, name="back_first")
         back_pair = ps.tile([P, 2, G], F32, name="back_pair")
         backs = [back_first[:], back_pair[:, 0, :], back_pair[:, 1, :]]
@@ -146,7 +145,7 @@ def tile_attend_filterconv_pl_kernel(tc, rad, wr, atom, wo, offs, out_0, out_1, 
                         )
                 continue
             if n == 2:
-                cast_wo(0)
+                cast_wo(0, slice(0, 4))
             sums = ps.tile([P, P], F32, name="sums", tag="sums", bufs=2)
             for e in range(EDGES):
                 nc.tensor.matmul(
@@ -157,8 +156,9 @@ def tile_attend_filterconv_pl_kernel(tc, rad, wr, atom, wo, offs, out_0, out_1, 
             if n == 0:
                 nc.scalar.copy(b_bf[:, :, 2:4], back_first[:].unsqueeze(2).to_broadcast([P, G, 2]))
             if n == 2:
-                cast_wo(1)
+                cast_wo(1, slice(0, 2))
                 nc.scalar.copy(b_bf[:, :, 0:2], back_pair[:].rearrange("p t g -> p g t"))
+                cast_wo(1, slice(2, 4))
 
         def quantise_wo(u, tag):
             codes = sb.tile([P, 2 * P], U32, name="wo_codes%d" % u, align_bytes=64)

@@ -160,33 +160,36 @@ def tile_attend_filterconv_pl_kernel(tc, rad, wr, atom, wo, offs, out_0, out_1, 
                 nc.scalar.copy(b_bf[:, :, 0:2], back_pair[:].rearrange("p t g -> p g t"))
                 cast_wo(1, slice(2, 4))
 
-        def quantise_wo(u, tag):
-            codes = sb.tile([P, 2 * P], U32, name="wo_codes%d" % u, align_bytes=64)
-            scales = sb.tile([P, 2 * P], U8, name="wo_scales%d" % u, tag=tag, align_bytes=64)
-            nc.vector.quantize_mx(
-                out=codes[:].bitcast(FP8X4), scales=scales[:], in_=wo_bf[:, u * 2 * P * PACK : (u + 1) * 2 * P * PACK]
-            )
-            return codes, scales
+        wo_q = []
 
-        wo_q = [quantise_wo(0, "wo_scales0")]
+        def quantise_wo(t, tag):
+            codes = sb.tile([P, P], U32, name="wo_codes%d" % t, align_bytes=64)
+            scales = sb.tile([P, P], U8, name="wo_scales%d" % t, tag=tag, align_bytes=64)
+            nc.vector.quantize_mx(
+                out=codes[:].bitcast(FP8X4), scales=scales[:], in_=wo_bf[:, t * P * PACK : (t + 1) * P * PACK]
+            )
+            wo_q.append((codes, scales))
+
+        quantise_wo(0, "wo_scales0")
         b_codes = sb.tile([P, G], U32, name="b_codes", align_bytes=64)
         b_scales = sb.tile([P, G], U8, name="b_scales", align_bytes=64)
         nc.vector.quantize_mx(
             out=b_codes[:].bitcast(FP8X4), scales=b_scales[:], in_=b_bf[:].rearrange("p g t -> p (g t)")
         )
-        wo_q.append(quantise_wo(1, "b_bf"))
+        quantise_wo(1, "b_bf")
+        quantise_wo(2, "wo_scales2")
+        quantise_wo(3, "wo_scales3")
         y = sb.tile([P, PACK, G], F32, name="y")
         for t in range(PACK):
-            codes, scales = wo_q[t // 2]
-            cols = slice((t % 2) * P, (t % 2 + 1) * P)
+            codes, scales = wo_q[t]
             if t < 3:
                 bank = ps.tile([P, HALF], F32, name="mm", tag="mm", bufs=3)
             else:
                 bank = ps.tile([P, HALF], F32, name="mm_last")
             nc.tensor.matmul_mx(
                 out=bank[:, :G],
-                lhsT=codes[:, cols].bitcast(FP8X4),
-                lhsT_scale=scales[:, cols],
+                lhsT=codes[:].bitcast(FP8X4),
+                lhsT_scale=scales[:],
                 rhs=b_codes[:].bitcast(FP8X4),
                 rhs_scale=b_scales[:],
                 start=True,
@@ -196,12 +199,20 @@ def tile_attend_filterconv_pl_kernel(tc, rad, wr, atom, wo, offs, out_0, out_1, 
         nc.sync.dma_start(out_0.rearrange("(p t) g -> p t g", t=PACK), y[:])
 
         y_bf = sb.tile([P, G * PACK], BF16, name="y_bf", align_bytes=64)
-        nc.vector.tensor_copy(
-            y_bf[:].rearrange("p (c i t) -> p c t i", i=4, t=PACK), y[:].rearrange("p t (c i) -> p c t i", i=4)
-        )
+        y_dst = y_bf[:].rearrange("p (c i t) -> p c t i", i=4, t=PACK)
+        y_src = y[:].rearrange("p t (c i) -> p c t i", i=4)
         y_codes = sb.tile([P, G], U32, name="y_codes", align_bytes=64)
         y_scales = sb.tile([P, G], U8, name="y_scales", align_bytes=64)
-        nc.vector.quantize_mx(out=y_codes[:].bitcast(FP8X4), scales=y_scales[:], in_=y_bf[:])
+        for h in range(2):
+            groups = slice(h * G // 8, (h + 1) * G // 8)
+            nc.vector.tensor_copy(y_dst[:, groups, :, :], y_src[:, groups, :, :])
+        for h in range(2):
+            cols = slice(h * G // 2, (h + 1) * G // 2)
+            nc.vector.quantize_mx(
+                out=y_codes[:, cols].bitcast(FP8X4),
+                scales=y_scales[:, cols],
+                in_=y_bf[:, h * G * PACK // 2 : (h + 1) * G * PACK // 2],
+            )
         nc.sync.dma_start(out_1[0].rearrange("l c r -> l (c r)").bitcast(I32), y_codes[:].bitcast(I32))
         scale_rows = out_2[0].bitcast(I32)
         for q in range(4):

@@ -23,6 +23,7 @@ HALF = I // 2
 WR_SPLIT = 88
 RAD_SPLIT = 344
 WO_CUTS = (0, 64, 128)
+WO_EARLY = 32
 ORDER = (2, 0, 1, 3)
 
 
@@ -84,37 +85,46 @@ def tile_attend_filterconv_pl_kernel(tc, rad, wr, atom, wo, offs, out_0, out_1, 
             nc.scalar.copy(dst[:, RAD_SPLIT // 4 :, :, :], src[:, RAD_SPLIT // 4 :, :, :])
             codes = sb.tile([P, HALF], U32, name="rad_codes%d" % h, align_bytes=64)
             scales = sb.tile([P, HALF], U8, name="rad_scales%d" % h, align_bytes=64)
-            nc.vector.quantize_mx(out=codes[:].bitcast(FP8X4), scales=scales[:], in_=rad_bf[:])
+            step = HALF // (h + 1)
+            for lo in range(0, HALF, step):
+                nc.vector.quantize_mx(
+                    out=codes[:, lo : lo + step].bitcast(FP8X4),
+                    scales=scales[:, lo : lo + step],
+                    in_=rad_bf[:, lo * PACK : (lo + step) * PACK],
+                )
             rad_codes.append(codes)
             rad_scales.append(scales)
 
-        def filters(t, h):
+        def filters(t, h, lo=0, hi=HALF):
             bank = ps.tile([P, HALF], F32, name="mm", tag="mm", bufs=3)
             cols = slice(t * P, (t + 1) * P)
             nc.tensor.matmul_mx(
-                out=bank[:],
+                out=bank[:, : hi - lo],
                 lhsT=wr_codes[:, cols].bitcast(FP8X4),
                 lhsT_scale=wr_scales[:, cols],
-                rhs=rad_codes[h][:].bitcast(FP8X4),
-                rhs_scale=rad_scales[h][:],
+                rhs=rad_codes[h][:, lo:hi].bitcast(FP8X4),
+                rhs_scale=rad_scales[h][:, lo:hi],
                 start=True,
                 stop=True,
             )
-            nc.scalar.copy(z[t][:, h * HALF : (h + 1) * HALF], bank[:])
+            nc.scalar.copy(z[t][:, h * HALF + lo : h * HALF + hi], bank[:, : hi - lo])
 
         quantise_rad(0)
         quantise_rad(1)
-        for t in ORDER:
+        filters(ORDER[0], 0)
+        filters(ORDER[0], 1, 0, HALF // 2)
+        filters(ORDER[0], 1, HALF // 2, HALF)
+        for t in ORDER[1:]:
             for h in range(2):
                 filters(t, h)
 
         b_bf = sb.tile([P, G, PACK], BF16, name="b_bf", tag="b_bf", align_bytes=64)
         wo_bf = wo_area[:, :I].bitcast(BF16)
-        wo_dst = wo_bf[:].rearrange("p (t m j) -> p m t j", t=PACK, j=PACK)
+        wo_dst = wo_bf[:].rearrange("p (t m j) -> p m j t", t=PACK, j=PACK)
 
-        def cast_wo(n, tiles):
-            src = wo_raw[n].rearrange("p j (m t) -> p m t j", t=PACK)
-            nc.scalar.copy(wo_dst[:, WO_CUTS[n] : WO_CUTS[n + 1], tiles, :], src[:, :, tiles, :])
+        def cast_wo(n, lo, hi, tiles):
+            src = wo_raw[n].rearrange("p j (m t) -> p m j t", t=PACK)
+            nc.scalar.copy(wo_dst[:, lo:hi, :, tiles], src[:, lo - WO_CUTS[n] : hi - WO_CUTS[n], :, tiles])
 
         sums_first = sb.tile([P, P], F32, name="sums_first")
         sums_second = sb.tile([P, P], F32, name="sums_second")
@@ -145,7 +155,8 @@ def tile_attend_filterconv_pl_kernel(tc, rad, wr, atom, wo, offs, out_0, out_1, 
                         )
                 continue
             if n == 2:
-                cast_wo(0, slice(0, 4))
+                cast_wo(0, 0, 64, slice(0, 2))
+                cast_wo(0, 0, WO_EARLY, slice(2, 4))
             sums = ps.tile([P, P], F32, name="sums", tag="sums", bufs=2)
             for e in range(EDGES):
                 nc.tensor.matmul(
@@ -156,9 +167,10 @@ def tile_attend_filterconv_pl_kernel(tc, rad, wr, atom, wo, offs, out_0, out_1, 
             if n == 0:
                 nc.scalar.copy(b_bf[:, :, 2:4], back_first[:].unsqueeze(2).to_broadcast([P, G, 2]))
             if n == 2:
-                cast_wo(1, slice(0, 2))
+                cast_wo(1, 64, 128, slice(0, 2))
                 nc.scalar.copy(b_bf[:, :, 0:2], back_pair[:].rearrange("p t g -> p g t"))
-                cast_wo(1, slice(2, 4))
+                cast_wo(0, WO_EARLY, 64, slice(2, 4))
+                cast_wo(1, 64, 128, slice(2, 4))
 
         wo_q = []
 

@@ -47,9 +47,10 @@ def tile_attend_filterconv_pl_kernel(tc, rad, wr, atom, wo, offs, out_0, out_1, 
         atom_rows = atom.rearrange("(p t) n -> p t n", t=PACK)
         wo_rows = wo.rearrange("(p j) f -> p j f", j=PACK)
         atoms = [sb.tile([P, T], F32, name="atom%d" % t) for t in range(PACK)]
-        wo_area = sb.tile([P, 2 * I], F32, name="wo_area", align_bytes=64)
+        wo_area = sb.tile([P, 2 * I + 3 * P], F32, name="wo_area", align_bytes=64)
+        wo_first = wo_area[:, :I]
         wo_second = sb.tile([P, PACK, F // 2], F32, name="wo_second")
-        wo_raw = [wo_area[:, I:].rearrange("p (j f) -> p j f", j=PACK), wo_second[:]]
+        wo_raw = [wo_first.rearrange("p (j f) -> p j f", j=PACK), wo_second[:]]
 
         def load_wo(n):
             nc.sync.dma_start(wo_raw[n], wo_rows[:, :, PACK * WO_CUTS[n] : PACK * WO_CUTS[n + 1]])
@@ -73,8 +74,10 @@ def tile_attend_filterconv_pl_kernel(tc, rad, wr, atom, wo, offs, out_0, out_1, 
         nc.vector.quantize_mx(out=wr_codes[:].bitcast(FP8X4), scales=wr_scales[:], in_=wr_bf[:])
 
         z = [
-            sb.tile([P, I], F32, name="z%d" % t, tag="rad_raw1" if t == ORDER[0] else "z%d" % t) for t in range(PACK)
+            sb.tile([P, I], F32, name="z%d" % t, tag="rad_raw1" if t == ORDER[0] else "z%d" % t)[:]
+            for t in range(PACK - 1)
         ]
+        z.append(wo_area[:, I + 3 * P :])
         rad_codes, rad_scales = [], []
 
         def quantise_rad(h):
@@ -119,12 +122,13 @@ def tile_attend_filterconv_pl_kernel(tc, rad, wr, atom, wo, offs, out_0, out_1, 
                 filters(t, h)
 
         b_bf = sb.tile([P, G, PACK], BF16, name="b_bf", tag="b_bf", align_bytes=64)
-        wo_bf = wo_area[:, :I].bitcast(BF16)
-        wo_dst = wo_bf[:].rearrange("p (t m j) -> p m j t", t=PACK, j=PACK)
+        wo_low = sb.tile([P, 2 * P * PACK], BF16, name="wo_low", align_bytes=64)
+        wo_bf = [wo_low[:], wo_area[:, I : I + 4 * P].bitcast(BF16)]
 
-        def cast_wo(n, lo, hi, tiles):
+        def cast_wo(n, lo, hi, u):
             src = wo_raw[n].rearrange("p j (m t) -> p m j t", t=PACK)
-            nc.scalar.copy(wo_dst[:, lo:hi, :, tiles], src[:, lo - WO_CUTS[n] : hi - WO_CUTS[n], :, tiles])
+            dst = wo_bf[u].rearrange("p (t m j) -> p m j t", t=2, j=PACK)
+            nc.scalar.copy(dst[:, lo:hi], src[:, lo - WO_CUTS[n] : hi - WO_CUTS[n], :, 2 * u : 2 * u + 2])
 
         sums_first = sb.tile([P, P], F32, name="sums_first")
         sums_second = sb.tile([P, P], F32, name="sums_second")
@@ -135,7 +139,7 @@ def tile_attend_filterconv_pl_kernel(tc, rad, wr, atom, wo, offs, out_0, out_1, 
         for n, t in enumerate(ORDER):
             x = sb.tile([P, I], F32, name="x%d" % t, tag="rad_bf1" if n == 0 else "x%d" % t, align_bytes=64)
             if n in (0, PACK - 1):
-                for h in range(2):
+                for h in (0, 1) if n == 0 else (1, 0):
                     nc.vector.tensor_tensor(
                         x[:, h * HALF : (h + 1) * HALF],
                         atoms[t][:].indirect(offsets[:, h * (HALF // 16) : (h + 1) * (HALF // 16)]),
@@ -146,17 +150,25 @@ def tile_attend_filterconv_pl_kernel(tc, rad, wr, atom, wo, offs, out_0, out_1, 
                 nc.vector.tensor_tensor(x[:], atoms[t][:].indirect(offsets[:]), z[t][:], MULT)
             if n == PACK - 1:
                 with nc.allow_low_precision(reason="float32 sum, rounded once to bfloat16 for the quantiser"):
-                    for h in range(2):
+                    for h in (1, 0):
                         nc.vector.tensor_reduce(
                             out=b_bf[:, h * (G // 2) : (h + 1) * (G // 2), t],
                             in_=x[:, h * HALF : (h + 1) * HALF].rearrange("p (g e) -> p g e", e=EDGES),
                             axis=mybir.AxisListType.X,
                             op=ADD,
                         )
+                nc.gpsimd.tensor_scalar(
+                    wo_bf[1].rearrange("p (t m j) -> p m t j", t=2, j=PACK)[:, 64:],
+                    wo_raw[1].rearrange("p j (m t) -> p m t j", t=PACK)[:, :, 2:4, :],
+                    1.0,
+                    0.0,
+                    MULT,
+                    ADD,
+                )
                 continue
             if n == 2:
-                cast_wo(0, 0, 64, slice(0, 2))
-                cast_wo(0, 0, WO_EARLY, slice(2, 4))
+                cast_wo(0, 0, 64, 0)
+                cast_wo(0, WO_EARLY, 64, 1)
             sums = ps.tile([P, P], F32, name="sums", tag="sums", bufs=2)
             for e in range(EDGES):
                 nc.tensor.matmul(
@@ -167,10 +179,9 @@ def tile_attend_filterconv_pl_kernel(tc, rad, wr, atom, wo, offs, out_0, out_1, 
             if n == 0:
                 nc.scalar.copy(b_bf[:, :, 2:4], back_first[:].unsqueeze(2).to_broadcast([P, G, 2]))
             if n == 2:
-                cast_wo(1, 64, 128, slice(0, 2))
+                cast_wo(1, 64, 128, 0)
                 nc.scalar.copy(b_bf[:, :, 0:2], back_pair[:].rearrange("p t g -> p g t"))
-                cast_wo(0, WO_EARLY, 64, slice(2, 4))
-                cast_wo(1, 64, 128, slice(2, 4))
+                cast_wo(0, 0, WO_EARLY, 1)
 
         wo_q = []
 
@@ -178,7 +189,7 @@ def tile_attend_filterconv_pl_kernel(tc, rad, wr, atom, wo, offs, out_0, out_1, 
             codes = sb.tile([P, P], U32, name="wo_codes%d" % t, align_bytes=64)
             scales = sb.tile([P, P], U8, name="wo_scales%d" % t, tag=tag, align_bytes=64)
             nc.vector.quantize_mx(
-                out=codes[:].bitcast(FP8X4), scales=scales[:], in_=wo_bf[:, t * P * PACK : (t + 1) * P * PACK]
+                out=codes[:].bitcast(FP8X4), scales=scales[:], in_=wo_bf[t // 2][:, t % 2 * P * PACK : (t % 2 + 1) * P * PACK]
             )
             wo_q.append((codes, scales))
 
@@ -188,7 +199,7 @@ def tile_attend_filterconv_pl_kernel(tc, rad, wr, atom, wo, offs, out_0, out_1, 
         nc.vector.quantize_mx(
             out=b_codes[:].bitcast(FP8X4), scales=b_scales[:], in_=b_bf[:].rearrange("p g t -> p (g t)")
         )
-        quantise_wo(1, "b_bf")
+        quantise_wo(1, "wo_scales1")
         quantise_wo(2, "wo_scales2")
         quantise_wo(3, "wo_scales3")
         y = sb.tile([P, PACK, G], F32, name="y")
@@ -215,9 +226,10 @@ def tile_attend_filterconv_pl_kernel(tc, rad, wr, atom, wo, offs, out_0, out_1, 
         y_src = y[:].rearrange("p t (c i) -> p c t i", i=4)
         y_codes = sb.tile([P, G], U32, name="y_codes", align_bytes=64)
         y_scales = sb.tile([P, G], U8, name="y_scales", align_bytes=64)
+        nc.vector.tensor_copy(y_dst[:, :, 0:2, :], y_src[:, :, 0:2, :])
         for h in range(2):
             groups = slice(h * G // 8, (h + 1) * G // 8)
-            nc.vector.tensor_copy(y_dst[:, groups, :, :], y_src[:, groups, :, :])
+            nc.vector.tensor_copy(y_dst[:, groups, 2:4, :], y_src[:, groups, 2:4, :])
         for h in range(2):
             cols = slice(h * G // 2, (h + 1) * G // 2)
             nc.vector.quantize_mx(

@@ -158,8 +158,8 @@ def tile_attend_filterconv_pl_kernel(tc, rad, wr, atom, wo, offs, out_0, out_1, 
                             op=ADD,
                         )
                 nc.gpsimd.tensor_scalar(
-                    wo_bf[1].rearrange("p (t m j) -> p m t j", t=2, j=PACK)[:, 64:],
-                    wo_raw[1].rearrange("p j (m t) -> p m t j", t=PACK)[:, :, 2:4, :],
+                    wo_bf[1].rearrange("p (t m j) -> p m j t", t=2, j=PACK)[:, 64:],
+                    wo_raw[1].rearrange("p j (m t) -> p m j t", t=PACK)[:, :, :, 2:4],
                     1.0,
                     0.0,
                     MULT,

@@ -15,16 +15,17 @@ U8 = mybir.dt.uint8
 FP8X4 = mybir.dt.float8_e4m3fn_x4
 MULT = mybir.AluOpType.mult
 ADD = mybir.AluOpType.add
+COPY = mybir.ActivationFunctionType.Copy
 
 P = 128
 PACK = 4
 EDGES = I // G
 HALF = I // 2
+PIECE = I // 4
 WR_SPLIT = 88
 RAD_SPLIT = 344
-WO_CUTS = (0, 64, 128)
-WO_EARLY = 32
 ORDER = (2, 0, 1, 3)
+BACK_AFTER = 2
 
 
 def tile_attend_filterconv_pl_kernel(tc, rad, wr, atom, wo, offs, out_0, out_1, out_2):
@@ -34,7 +35,6 @@ def tile_attend_filterconv_pl_kernel(tc, rad, wr, atom, wo, offs, out_0, out_1, 
         ps = ctx.enter_context(tc.psum_pool(name="ps", bufs=1))
 
         offsets = sb.tile([P, I // 16], U16, name="offsets")
-
         wr_raw = sb.tile([P, PACK, K], F32, name="wr_raw")
         nc.sync.dma_start(wr_raw[:], wr.rearrange("(p j) k -> p j k", j=PACK))
         rad_rows = rad.rearrange("(p j) i -> p j i", j=PACK)
@@ -45,24 +45,22 @@ def tile_attend_filterconv_pl_kernel(tc, rad, wr, atom, wo, offs, out_0, out_1, 
             rad_raw.append(raw)
         nc.sync.dma_start(offsets[:], offs)
         atom_rows = atom.rearrange("(p t) n -> p t n", t=PACK)
+        atoms = []
+        for t in ORDER:
+            raw = sb.tile([P, T], F32, name="atom%d" % t, tag="atom%d" % t, align_bytes=64)
+            nc.sync.dma_start(raw[:], atom_rows[:, t, :])
+            atoms.append(raw)
         wo_rows = wo.rearrange("(p j) f -> p j f", j=PACK)
-        atoms = [sb.tile([P, T], F32, name="atom%d" % t) for t in range(PACK)]
-        wo_area = sb.tile([P, 2 * I + 3 * P], F32, name="wo_area", align_bytes=64)
-        wo_first = wo_area[:, :I]
-        wo_second = sb.tile([P, PACK, F // 2], F32, name="wo_second")
-        wo_raw = [wo_first.rearrange("p (j f) -> p j f", j=PACK), wo_second[:]]
-
-        def load_wo(n):
-            nc.sync.dma_start(wo_raw[n], wo_rows[:, :, PACK * WO_CUTS[n] : PACK * WO_CUTS[n + 1]])
-
-        for t in ORDER[:-1]:
-            nc.sync.dma_start(atoms[t][:], atom_rows[:, t, :])
-        nc.sync.dma_start(atoms[PACK - 1][:], atom_rows[:, PACK - 1, :])
-        load_wo(0)
-        load_wo(1)
+        wo_raw = []
+        for h in range(2):
+            raw = sb.tile([P, PACK, F // 2], F32, name="wo_raw%d" % h)
+            nc.sync.dma_start(raw[:], wo_rows[:, :, h * F // 2 : (h + 1) * F // 2])
+            wo_raw.append(raw)
 
         ident = sb.tile([P, P], F32, name="ident")
         make_identity(nc, ident[:])
+
+        banks = [ps.tile([P, HALF], F32, name="bank%d" % n) for n in range(8)]
 
         wr_bf = sb.tile([P, K * PACK], BF16, name="wr_bf", align_bytes=64)
         wr_dst = wr_bf[:].rearrange("p (t m j) -> p m t j", t=PACK, j=PACK)
@@ -73,142 +71,159 @@ def tile_attend_filterconv_pl_kernel(tc, rad, wr, atom, wo, offs, out_0, out_1, 
         wr_scales = sb.tile([P, K], U8, name="wr_scales", align_bytes=64)
         nc.vector.quantize_mx(out=wr_codes[:].bitcast(FP8X4), scales=wr_scales[:], in_=wr_bf[:])
 
-        z = [
-            sb.tile([P, I], F32, name="z%d" % t, tag="rad_raw1" if t == ORDER[0] else "z%d" % t)[:]
-            for t in range(PACK - 1)
-        ]
-        z.append(wo_area[:, I + 3 * P :])
+        area = sb.tile([P, 3 * I], F32, name="area", align_bytes=64)
+        rad_first = sb.tile([P, HALF * PACK], BF16, name="rad_first", align_bytes=64)
+        rad_bf = [rad_first[:], area[:, I + PIECE : 2 * I + PIECE].bitcast(BF16)]
         rad_codes, rad_scales = [], []
-
-        def quantise_rad(h):
-            rad_bf = sb.tile([P, HALF * PACK], BF16, name="rad_bf%d" % h, tag="rad_bf%d" % h, align_bytes=64)
-            dst = rad_bf[:].rearrange("p (c i j) -> p c j i", i=4, j=PACK)
+        for h in range(2):
+            dst = rad_bf[h].rearrange("p (c i j) -> p c j i", i=4, j=PACK)
             src = rad_raw[h][:].rearrange("p j (c i) -> p c j i", i=4)
             nc.vector.tensor_copy(dst[:, : RAD_SPLIT // 4, :, :], src[:, : RAD_SPLIT // 4, :, :])
             nc.scalar.copy(dst[:, RAD_SPLIT // 4 :, :, :], src[:, RAD_SPLIT // 4 :, :, :])
             codes = sb.tile([P, HALF], U32, name="rad_codes%d" % h, align_bytes=64)
             scales = sb.tile([P, HALF], U8, name="rad_scales%d" % h, align_bytes=64)
-            step = HALF // (h + 1)
-            for lo in range(0, HALF, step):
-                nc.vector.quantize_mx(
-                    out=codes[:, lo : lo + step].bitcast(FP8X4),
-                    scales=scales[:, lo : lo + step],
-                    in_=rad_bf[:, lo * PACK : (lo + step) * PACK],
-                )
+            nc.vector.quantize_mx(out=codes[:].bitcast(FP8X4), scales=scales[:], in_=rad_bf[h])
             rad_codes.append(codes)
             rad_scales.append(scales)
 
-        def filters(t, h, lo=0, hi=HALF):
-            bank = ps.tile([P, HALF], F32, name="mm", tag="mm", bufs=3)
-            cols = slice(t * P, (t + 1) * P)
+        def filter_bank(n, h):
+            return banks[n] if h == 1 else banks[4 + n]
+
+        def filters(n, h):
+            cols = slice(ORDER[n] * P, (ORDER[n] + 1) * P)
             nc.tensor.matmul_mx(
-                out=bank[:, : hi - lo],
+                out=filter_bank(n, h)[:],
                 lhsT=wr_codes[:, cols].bitcast(FP8X4),
                 lhsT_scale=wr_scales[:, cols],
-                rhs=rad_codes[h][:, lo:hi].bitcast(FP8X4),
-                rhs_scale=rad_scales[h][:, lo:hi],
+                rhs=rad_codes[h][:].bitcast(FP8X4),
+                rhs_scale=rad_scales[h][:],
                 start=True,
                 stop=True,
             )
-            nc.scalar.copy(z[t][:, h * HALF + lo : h * HALF + hi], bank[:, : hi - lo])
 
-        quantise_rad(0)
-        quantise_rad(1)
-        filters(ORDER[0], 0)
-        filters(ORDER[0], 1, 0, HALF // 2)
-        filters(ORDER[0], 1, HALF // 2, HALF)
-        for t in ORDER[1:]:
-            for h in range(2):
-                filters(t, h)
+        fused = [HALF, HALF, HALF, PIECE]
+        third = sb.tile([P, I + HALF], F32, name="third", tag="rad_raw1")
+        x = [area[:, 2 * I :], area[:, I : 2 * I], third[:, :I]]
+        z = [third[:, :HALF], third[:, I:]]
+        last = PACK - 1
+        picked = {(n, HALF): x[n + 1][:, :HALF] for n in range(2)}
+        for q in range(1, 4):
+            picked[(last, q * PIECE)] = x[0][:, q * PIECE : (q + 1) * PIECE]
 
-        b_bf = sb.tile([P, G, PACK], BF16, name="b_bf", tag="b_bf", align_bytes=64)
-        wo_low = sb.tile([P, 2 * P * PACK], BF16, name="wo_low", align_bytes=64)
-        wo_bf = [wo_low[:], wo_area[:, I : I + 4 * P].bitcast(BF16)]
+        def empty_filters(n):
+            nc.scalar.copy(z[n], filter_bank(n, 0)[:, : fused[n]])
 
-        def cast_wo(n, lo, hi, u):
-            src = wo_raw[n].rearrange("p j (m t) -> p m j t", t=PACK)
-            dst = wo_bf[u].rearrange("p (t m j) -> p m j t", t=2, j=PACK)
-            nc.scalar.copy(dst[:, lo:hi], src[:, lo - WO_CUTS[n] : hi - WO_CUTS[n], :, 2 * u : 2 * u + 2])
+        def window(n, lo, hi):
+            return atoms[n][:].indirect(offsets[:, lo // 16 : hi // 16])
+
+        def fused_product(n):
+            nc.vector.tensor_tensor(x[n][:, : fused[n]], window(n, 0, fused[n]), z[n], MULT)
+
+        def pick(n, lo, hi):
+            nc.scalar.activation(picked[(n, lo)], window(n, lo, hi), COPY)
+
+        def product(n, lo, hi):
+            h = lo // HALF
+            nc.vector.tensor_tensor(
+                x[n][:, lo:hi], picked[(n, lo)], filter_bank(n, h)[:, lo - h * HALF : hi - h * HALF], MULT
+            )
 
         sums_first = sb.tile([P, P], F32, name="sums_first")
-        sums_second = sb.tile([P, P], F32, name="sums_second")
-        sums_sb = [sums_first[:], sums_second[:], wo_area[:, I - P // 2 : I + P // 2]]
-        back_first = ps.tile([P, G], F32, name="back_first")
-        back_pair = ps.tile([P, 2, G], F32, name="back_pair")
-        backs = [back_first[:], back_pair[:, 0, :], back_pair[:, 1, :]]
-        for n, t in enumerate(ORDER):
-            x = sb.tile([P, I], F32, name="x%d" % t, tag="rad_bf1" if n == 0 else "x%d" % t, align_bytes=64)
-            if n in (0, PACK - 1):
-                for h in (0, 1) if n == 0 else (1, 0):
-                    nc.vector.tensor_tensor(
-                        x[:, h * HALF : (h + 1) * HALF],
-                        atoms[t][:].indirect(offsets[:, h * (HALF // 16) : (h + 1) * (HALF // 16)]),
-                        z[t][:, h * HALF : (h + 1) * HALF],
-                        MULT,
-                    )
-            else:
-                nc.vector.tensor_tensor(x[:], atoms[t][:].indirect(offsets[:]), z[t][:], MULT)
-            if n == PACK - 1:
-                with nc.allow_low_precision(reason="float32 sum, rounded once to bfloat16 for the quantiser"):
-                    for h in (1, 0):
-                        nc.vector.tensor_reduce(
-                            out=b_bf[:, h * (G // 2) : (h + 1) * (G // 2), t],
-                            in_=x[:, h * HALF : (h + 1) * HALF].rearrange("p (g e) -> p g e", e=EDGES),
-                            axis=mybir.AxisListType.X,
-                            op=ADD,
-                        )
-                nc.gpsimd.tensor_scalar(
-                    wo_bf[1].rearrange("p (t m j) -> p m j t", t=2, j=PACK)[:, 64:],
-                    wo_raw[1].rearrange("p j (m t) -> p m j t", t=PACK)[:, :, :, 2:4],
-                    1.0,
-                    0.0,
-                    MULT,
-                    ADD,
-                )
-                continue
-            if n == 2:
-                cast_wo(0, 0, 64, 0)
-                cast_wo(0, WO_EARLY, 64, 1)
-            sums = ps.tile([P, P], F32, name="sums", tag="sums", bufs=2)
-            for e in range(EDGES):
+        sums_pair = sb.tile([P, 2 * P], F32, name="sums_pair")
+        sum_banks = [banks[4][:, :P], banks[0][:, :P], banks[0][:, P : 2 * P]]
+        backs = [banks[1][:, :G], banks[2][:, :G], banks[2][:, G : 2 * G]]
+
+        def edge_sums(n, edges):
+            for e in edges:
                 nc.tensor.matmul(
-                    sums[:], x[:, e:I:EDGES], ident[:], start=(e == 0), stop=(e == EDGES - 1), is_transpose=True
+                    sum_banks[n],
+                    x[n][:, e:I:EDGES],
+                    ident[:],
+                    start=(e == 0),
+                    stop=(e == EDGES - 1),
+                    is_transpose=True,
                 )
-            nc.scalar.copy(sums_sb[n], sums[:])
-            nc.tensor.transpose(backs[n], sums_sb[n], ident[:])
+
+        for h in range(2):
+            for n in range(PACK):
+                filters(n, h)
+        empty_filters(0)
+        empty_filters(1)
+        for n in range(last):
+            fused_product(n)
+            pick(n, HALF, I)
             if n == 0:
-                nc.scalar.copy(b_bf[:, :, 2:4], back_first[:].unsqueeze(2).to_broadcast([P, G, 2]))
+                third_filters = sb.tile([P, HALF], F32, name="third_filters", tag="atom%d" % ORDER[0], align_bytes=64)
+                z.append(third_filters[:])
+                empty_filters(2)
+            if n == 1:
+                fourth = sb.tile([P, I + PIECE], F32, name="fourth", tag="atom%d" % ORDER[1], align_bytes=64)
+                x.append(fourth[:, :I])
+                z.append(fourth[:, I:])
+                picked[(2, HALF)] = fourth[:, :HALF]
+                empty_filters(3)
             if n == 2:
-                cast_wo(1, 64, 128, 0)
-                nc.scalar.copy(b_bf[:, :, 0:2], back_pair[:].rearrange("p t g -> p g t"))
-                cast_wo(0, 0, WO_EARLY, 1)
+                b_bf = sb.tile([P, G, PACK], BF16, name="b_bf", tag="atom%d" % ORDER[0], align_bytes=64)
+                nc.scalar.copy(b_bf[:, :, 2:4], backs[0].unsqueeze(2).to_broadcast([P, G, 2]))
+            product(n, HALF, I)
+            edge_sums(n, range(BACK_AFTER))
+            if n == 1:
+                nc.tensor.transpose(backs[0], sums_first[:], ident[:])
+            edge_sums(n, range(BACK_AFTER, EDGES))
+            if n == 0:
+                nc.scalar.copy(sums_first[:], sum_banks[0])
+
+        def last_sums(q):
+            with nc.allow_low_precision(reason="float32 sum, rounded once to bfloat16 for the quantiser"):
+                nc.vector.tensor_reduce(
+                    out=b_bf[:, q * PIECE // EDGES : (q + 1) * PIECE // EDGES, ORDER[last]],
+                    in_=x[last][:, q * PIECE : (q + 1) * PIECE].rearrange("p (g e) -> p g e", e=EDGES),
+                    axis=mybir.AxisListType.X,
+                    op=ADD,
+                )
+
+        wo_bf = area[:, :I].bitcast(BF16)
+        wo_dst = wo_bf.rearrange("p (t m j) -> p m j t", t=PACK, j=PACK)
+        wo_src = [raw[:].rearrange("p j (m t) -> p m j t", t=PACK) for raw in wo_raw]
+
+        fused_product(last)
+        for q in range(1, 4):
+            pick(last, q * PIECE, (q + 1) * PIECE)
+        nc.scalar.copy(sums_pair[:], banks[0][:, : 2 * P])
+        for n in range(2):
+            nc.tensor.transpose(backs[1 + n], sums_pair[:, n * P : (n + 1) * P], ident[:])
+        for q in range(1, 4):
+            product(last, q * PIECE, (q + 1) * PIECE)
+            last_sums(q - 1)
+        nc.gpsimd.tensor_scalar(wo_dst[:, :64], wo_src[0], 1.0, 0.0, MULT, ADD)
+        for u in range(2):
+            nc.scalar.copy(wo_dst[:, 64:, :, 2 * u : 2 * u + 2], wo_src[1][:, :, :, 2 * u : 2 * u + 2])
+        last_sums(3)
+        nc.vector.tensor_copy(b_bf[:, :, 0:2], banks[2][:, : 2 * G].rearrange("p (t g) -> p g t", t=2))
 
         wo_q = []
 
-        def quantise_wo(t, tag):
+        def quantise_wo(t):
             codes = sb.tile([P, P], U32, name="wo_codes%d" % t, align_bytes=64)
-            scales = sb.tile([P, P], U8, name="wo_scales%d" % t, tag=tag, align_bytes=64)
+            scales = sb.tile([P, P], U8, name="wo_scales%d" % t, align_bytes=64)
             nc.vector.quantize_mx(
-                out=codes[:].bitcast(FP8X4), scales=scales[:], in_=wo_bf[t // 2][:, t % 2 * P * PACK : (t % 2 + 1) * P * PACK]
+                out=codes[:].bitcast(FP8X4), scales=scales[:], in_=wo_bf[:, t * P * PACK : (t + 1) * P * PACK]
             )
             wo_q.append((codes, scales))
 
-        quantise_wo(0, "wo_scales0")
+        quantise_wo(0)
+        quantise_wo(1)
         b_codes = sb.tile([P, G], U32, name="b_codes", align_bytes=64)
         b_scales = sb.tile([P, G], U8, name="b_scales", align_bytes=64)
         nc.vector.quantize_mx(
             out=b_codes[:].bitcast(FP8X4), scales=b_scales[:], in_=b_bf[:].rearrange("p g t -> p (g t)")
         )
-        quantise_wo(1, "wo_scales1")
-        quantise_wo(2, "wo_scales2")
-        quantise_wo(3, "wo_scales3")
+        for t in range(2, PACK):
+            quantise_wo(t)
         y = sb.tile([P, PACK, G], F32, name="y")
         for t in range(PACK):
             codes, scales = wo_q[t]
-            if t < 3:
-                bank = ps.tile([P, HALF], F32, name="mm", tag="mm", bufs=3)
-            else:
-                bank = ps.tile([P, HALF], F32, name="mm_last")
+            bank = banks[(4, 5, 6, 1)[t]]
             nc.tensor.matmul_mx(
                 out=bank[:, :G],
                 lhsT=codes[:].bitcast(FP8X4),

@@ -195,11 +195,25 @@ def tile_attend_filterconv_pl_kernel(tc, rad, wr, atom, wo, offs, out_0, out_1, 
         for q in range(1, 4):
             product(last, q * PIECE, (q + 1) * PIECE)
             last_sums(q - 1)
-        nc.gpsimd.tensor_scalar(wo_dst[:, :64], wo_src[0], 1.0, 0.0, MULT, ADD)
-        for u in range(2):
-            nc.scalar.copy(wo_dst[:, 64:, :, 2 * u : 2 * u + 2], wo_src[1][:, :, :, 2 * u : 2 * u + 2])
+        nc.gpsimd.tensor_scalar(
+            wo_bf.rearrange("p (t m j) -> p m t j", t=PACK, j=PACK)[:, :64],
+            wo_raw[0][:].rearrange("p j (m t) -> p m t j", t=PACK),
+            1.0,
+            0.0,
+            MULT,
+            ADD,
+        )
+        nc.gpsimd.tensor_scalar(
+            wo_bf.rearrange("p (t m j) -> p m t j", t=PACK, j=PACK)[:, 64:, 0:2],
+            wo_raw[1][:].rearrange("p j (m t) -> p m t j", t=PACK)[:, :, 0:2],
+            1.0,
+            0.0,
+            MULT,
+            ADD,
+        )
         last_sums(3)
-        nc.vector.tensor_copy(b_bf[:, :, 0:2], banks[2][:, : 2 * G].rearrange("p (t g) -> p g t", t=2))
+        nc.scalar.copy(b_bf[:, :, 0:2], banks[2][:, : 2 * G].rearrange("p (t g) -> p g t", t=2))
+        nc.scalar.copy(wo_dst[:, 64:, :, 2:4], wo_src[1][:, :, :, 2:4])
 
         wo_q = []
 

@@ -26,6 +26,7 @@ WR_SPLIT = 88
 RAD_SPLIT = 344
 ORDER = (2, 0, 1, 3)
 BACK_AFTER = 2
+WO_LATE = 24
 
 
 def tile_attend_filterconv_pl_kernel(tc, rad, wr, atom, wo, offs, out_0, out_1, out_2):
@@ -71,9 +72,9 @@ def tile_attend_filterconv_pl_kernel(tc, rad, wr, atom, wo, offs, out_0, out_1, 
         wr_scales = sb.tile([P, K], U8, name="wr_scales", align_bytes=64)
         nc.vector.quantize_mx(out=wr_codes[:].bitcast(FP8X4), scales=wr_scales[:], in_=wr_bf[:])
 
-        area = sb.tile([P, 3 * I], F32, name="area", align_bytes=64)
+        area = sb.tile([P, 3 * I + PIECE], F32, name="area", align_bytes=64)
         rad_first = sb.tile([P, HALF * PACK], BF16, name="rad_first", align_bytes=64)
-        rad_bf = [rad_first[:], area[:, I + PIECE : 2 * I + PIECE].bitcast(BF16)]
+        rad_bf = [rad_first[:], area[:, I + HALF : 2 * I + HALF].bitcast(BF16)]
         rad_codes, rad_scales = [], []
         for h in range(2):
             dst = rad_bf[h].rearrange("p (c i j) -> p c j i", i=4, j=PACK)
@@ -103,11 +104,12 @@ def tile_attend_filterconv_pl_kernel(tc, rad, wr, atom, wo, offs, out_0, out_1, 
 
         fused = [HALF, HALF, HALF, PIECE]
         third = sb.tile([P, I + HALF], F32, name="third", tag="rad_raw1")
-        x = [area[:, 2 * I :], area[:, I : 2 * I], third[:, :I]]
+        x = [area[:, 2 * I + PIECE :], area[:, I + PIECE : 2 * I + PIECE], third[:, :I]]
         z = [third[:, :HALF], third[:, I:]]
         last = PACK - 1
         picked = {(n, HALF): x[n + 1][:, :HALF] for n in range(2)}
-        for q in range(1, 4):
+        picked[(last, PIECE)] = area[:, I - 2 * WO_LATE : I - 2 * WO_LATE + PIECE]
+        for q in range(2, 4):
             picked[(last, q * PIECE)] = x[0][:, q * PIECE : (q + 1) * PIECE]
 
         def empty_filters(n):
@@ -129,7 +131,7 @@ def tile_attend_filterconv_pl_kernel(tc, rad, wr, atom, wo, offs, out_0, out_1, 
             )
 
         sums_first = sb.tile([P, P], F32, name="sums_first")
-        sums_pair = sb.tile([P, 2 * P], F32, name="sums_pair")
+        sums_pair = picked[(last, PIECE)]
         sum_banks = [banks[4][:, :P], banks[0][:, :P], banks[0][:, P : 2 * P]]
         backs = [banks[1][:, :G], banks[2][:, :G], banks[2][:, G : 2 * G]]
 
@@ -189,12 +191,12 @@ def tile_attend_filterconv_pl_kernel(tc, rad, wr, atom, wo, offs, out_0, out_1, 
         fused_product(last)
         for q in range(1, 4):
             pick(last, q * PIECE, (q + 1) * PIECE)
-        nc.scalar.copy(sums_pair[:], banks[0][:, : 2 * P])
-        for n in range(2):
-            nc.tensor.transpose(backs[1 + n], sums_pair[:, n * P : (n + 1) * P], ident[:])
         for q in range(1, 4):
             product(last, q * PIECE, (q + 1) * PIECE)
             last_sums(q - 1)
+        nc.scalar.copy(sums_pair, banks[0][:, : 2 * P])
+        for n in range(2):
+            nc.tensor.transpose(backs[1 + n], sums_pair[:, n * P : (n + 1) * P], ident[:])
         nc.gpsimd.tensor_scalar(
             wo_bf.rearrange("p (t m j) -> p m t j", t=PACK, j=PACK)[:, :64],
             wo_raw[0][:].rearrange("p j (m t) -> p m t j", t=PACK),
@@ -212,8 +214,9 @@ def tile_attend_filterconv_pl_kernel(tc, rad, wr, atom, wo, offs, out_0, out_1, 
             ADD,
         )
         last_sums(3)
+        nc.scalar.copy(wo_dst[:, 64 : P - WO_LATE, :, 2:4], wo_src[1][:, : 64 - WO_LATE, :, 2:4])
         nc.scalar.copy(b_bf[:, :, 0:2], banks[2][:, : 2 * G].rearrange("p (t g) -> p g t", t=2))
-        nc.scalar.copy(wo_dst[:, 64:, :, 2:4], wo_src[1][:, :, :, 2:4])
+        nc.scalar.copy(wo_dst[:, P - WO_LATE :, :, 2:4], wo_src[1][:, 64 - WO_LATE :, :, 2:4])
 
         wo_q = []
 

@@ -26,7 +26,7 @@ WR_SPLIT = 88
 RAD_SPLIT = 344
 ORDER = (2, 0, 1, 3)
 BACK_AFTER = 2
-WO_LATE = 24
+WO_LATE = 44
 
 
 def tile_attend_filterconv_pl_kernel(tc, rad, wr, atom, wo, offs, out_0, out_1, out_2):
@@ -72,9 +72,9 @@ def tile_attend_filterconv_pl_kernel(tc, rad, wr, atom, wo, offs, out_0, out_1, 
         wr_scales = sb.tile([P, K], U8, name="wr_scales", align_bytes=64)
         nc.vector.quantize_mx(out=wr_codes[:].bitcast(FP8X4), scales=wr_scales[:], in_=wr_bf[:])
 
-        area = sb.tile([P, 3 * I + PIECE], F32, name="area", align_bytes=64)
+        area = sb.tile([P, 3 * I + HALF], F32, name="area", align_bytes=64)
         rad_first = sb.tile([P, HALF * PACK], BF16, name="rad_first", align_bytes=64)
-        rad_bf = [rad_first[:], area[:, I + HALF : 2 * I + HALF].bitcast(BF16)]
+        rad_bf = [rad_first[:], area[:, I + 3 * PIECE : 2 * I + 3 * PIECE].bitcast(BF16)]
         rad_codes, rad_scales = [], []
         for h in range(2):
             dst = rad_bf[h].rearrange("p (c i j) -> p c j i", i=4, j=PACK)
@@ -104,13 +104,15 @@ def tile_attend_filterconv_pl_kernel(tc, rad, wr, atom, wo, offs, out_0, out_1, 
 
         fused = [HALF, HALF, HALF, PIECE]
         third = sb.tile([P, I + HALF], F32, name="third", tag="rad_raw1")
-        x = [area[:, 2 * I + PIECE :], area[:, I + PIECE : 2 * I + PIECE], third[:, :I]]
+        x = [area[:, 2 * I + HALF :], area[:, I + HALF : 2 * I + HALF], third[:, :I]]
         z = [third[:, :HALF], third[:, I:]]
         last = PACK - 1
         picked = {(n, HALF): x[n + 1][:, :HALF] for n in range(2)}
-        picked[(last, PIECE)] = area[:, I - 2 * WO_LATE : I - 2 * WO_LATE + PIECE]
-        for q in range(2, 4):
-            picked[(last, q * PIECE)] = x[0][:, q * PIECE : (q + 1) * PIECE]
+        pair_starts = (0, HALF + PIECE)
+        late_starts = [start + HALF - 2 * WO_LATE for start in pair_starts]
+        picked[(last, PIECE)] = area[:, late_starts[1] : late_starts[1] + PIECE]
+        picked[(last, 2 * PIECE)] = x[0][:, :PIECE]
+        picked[(last, 3 * PIECE)] = area[:, late_starts[0] : late_starts[0] + PIECE]
 
         def empty_filters(n):
             nc.scalar.copy(z[n], filter_bank(n, 0)[:, : fused[n]])
@@ -184,9 +186,13 @@ def tile_attend_filterconv_pl_kernel(tc, rad, wr, atom, wo, offs, out_0, out_1, 
                     op=ADD,
                 )
 
-        wo_bf = area[:, :I].bitcast(BF16)
-        wo_dst = wo_bf.rearrange("p (t m j) -> p m j t", t=PACK, j=PACK)
-        wo_src = [raw[:].rearrange("p j (m t) -> p m j t", t=PACK) for raw in wo_raw]
+        wo_bf = [area[:, start : start + HALF].bitcast(BF16) for start in pair_starts]
+
+        def wo_views(u, lo, hi, walk):
+            h = lo // 64
+            dst = wo_bf[u].rearrange("p (t m j) -> p " + walk, t=2, j=PACK)
+            src = wo_raw[h][:].rearrange("p j (m u t) -> p u " + walk, u=2, t=2)[:, u]
+            return dst[:, lo:hi], src[:, lo - 64 * h : hi - 64 * h]
 
         fused_product(last)
         for q in range(1, 4):
@@ -197,26 +203,14 @@ def tile_attend_filterconv_pl_kernel(tc, rad, wr, atom, wo, offs, out_0, out_1, 
         nc.scalar.copy(sums_pair, banks[0][:, : 2 * P])
         for n in range(2):
             nc.tensor.transpose(backs[1 + n], sums_pair[:, n * P : (n + 1) * P], ident[:])
-        nc.gpsimd.tensor_scalar(
-            wo_bf.rearrange("p (t m j) -> p m t j", t=PACK, j=PACK)[:, :64],
-            wo_raw[0][:].rearrange("p j (m t) -> p m t j", t=PACK),
-            1.0,
-            0.0,
-            MULT,
-            ADD,
-        )
-        nc.gpsimd.tensor_scalar(
-            wo_bf.rearrange("p (t m j) -> p m t j", t=PACK, j=PACK)[:, 64:, 0:2],
-            wo_raw[1][:].rearrange("p j (m t) -> p m t j", t=PACK)[:, :, 0:2],
-            1.0,
-            0.0,
-            MULT,
-            ADD,
-        )
+        for u in range(2):
+            nc.gpsimd.tensor_scalar(*wo_views(u, 0, 64, "m t j"), 1.0, 0.0, MULT, ADD)
         last_sums(3)
-        nc.scalar.copy(wo_dst[:, 64 : P - WO_LATE, :, 2:4], wo_src[1][:, : 64 - WO_LATE, :, 2:4])
+        nc.vector.tensor_copy(*wo_views(0, P - WO_LATE, P, "m j t"))
+        for u in range(2):
+            nc.scalar.copy(*wo_views(u, 64, P - WO_LATE, "m j t"))
         nc.scalar.copy(b_bf[:, :, 0:2], banks[2][:, : 2 * G].rearrange("p (t g) -> p g t", t=2))
-        nc.scalar.copy(wo_dst[:, P - WO_LATE :, :, 2:4], wo_src[1][:, 64 - WO_LATE :, :, 2:4])
+        nc.scalar.copy(*wo_views(1, P - WO_LATE, P, "m j t"))
 
         wo_q = []
 
@@ -224,18 +218,16 @@ def tile_attend_filterconv_pl_kernel(tc, rad, wr, atom, wo, offs, out_0, out_1, 
             codes = sb.tile([P, P], U32, name="wo_codes%d" % t, align_bytes=64)
             scales = sb.tile([P, P], U8, name="wo_scales%d" % t, align_bytes=64)
             nc.vector.quantize_mx(
-                out=codes[:].bitcast(FP8X4), scales=scales[:], in_=wo_bf[:, t * P * PACK : (t + 1) * P * PACK]
+                out=codes[:].bitcast(FP8X4), scales=scales[:], in_=wo_bf[t // 2][:, t % 2 * P * PACK : (t % 2 + 1) * P * PACK]
             )
             wo_q.append((codes, scales))
 
-        quantise_wo(0)
-        quantise_wo(1)
         b_codes = sb.tile([P, G], U32, name="b_codes", align_bytes=64)
         b_scales = sb.tile([P, G], U8, name="b_scales", align_bytes=64)
         nc.vector.quantize_mx(
             out=b_codes[:].bitcast(FP8X4), scales=b_scales[:], in_=b_bf[:].rearrange("p g t -> p (g t)")
         )
-        for t in range(2, PACK):
+        for t in range(PACK):
             quantise_wo(t)
         y = sb.tile([P, PACK, G], F32, name="y")
         for t in range(PACK):

@@ -26,7 +26,7 @@ WR_SPLIT = 88
 RAD_SPLIT = 344
 ORDER = (2, 0, 1, 3)
 BACK_AFTER = 2
-WO_LATE = 44
+WO_LATE = 32
 
 
 def tile_attend_filterconv_pl_kernel(tc, rad, wr, atom, wo, offs, out_0, out_1, out_2):
@@ -72,9 +72,9 @@ def tile_attend_filterconv_pl_kernel(tc, rad, wr, atom, wo, offs, out_0, out_1, 
         wr_scales = sb.tile([P, K], U8, name="wr_scales", align_bytes=64)
         nc.vector.quantize_mx(out=wr_codes[:].bitcast(FP8X4), scales=wr_scales[:], in_=wr_bf[:])
 
-        area = sb.tile([P, 3 * I + HALF], F32, name="area", align_bytes=64)
+        area = sb.tile([P, 3 * I], F32, name="area", align_bytes=64)
         rad_first = sb.tile([P, HALF * PACK], BF16, name="rad_first", align_bytes=64)
-        rad_bf = [rad_first[:], area[:, I + 3 * PIECE : 2 * I + 3 * PIECE].bitcast(BF16)]
+        rad_bf = [rad_first[:], area[:, I + PIECE : 2 * I + PIECE].bitcast(BF16)]
         rad_codes, rad_scales = [], []
         for h in range(2):
             dst = rad_bf[h].rearrange("p (c i j) -> p c j i", i=4, j=PACK)
@@ -104,12 +104,12 @@ def tile_attend_filterconv_pl_kernel(tc, rad, wr, atom, wo, offs, out_0, out_1, 
 
         fused = [HALF, HALF, HALF, PIECE]
         third = sb.tile([P, I + HALF], F32, name="third", tag="rad_raw1")
-        x = [area[:, 2 * I + HALF :], area[:, I + HALF : 2 * I + HALF], third[:, :I]]
+        x = [area[:, 2 * I :], area[:, I : 2 * I], third[:, :I]]
         z = [third[:, :HALF], third[:, I:]]
         last = PACK - 1
         picked = {(n, HALF): x[n + 1][:, :HALF] for n in range(2)}
-        pair_starts = (0, HALF + PIECE)
-        late_starts = [start + HALF - 2 * WO_LATE for start in pair_starts]
+        pair_starts = (0, HALF)
+        late_starts = [pair_starts[0] + P, pair_starts[1] + PIECE - 2 * WO_LATE]
         picked[(last, PIECE)] = area[:, late_starts[1] : late_starts[1] + PIECE]
         picked[(last, 2 * PIECE)] = x[0][:, :PIECE]
         picked[(last, 3 * PIECE)] = area[:, late_starts[0] : late_starts[0] + PIECE]
@@ -133,9 +133,9 @@ def tile_attend_filterconv_pl_kernel(tc, rad, wr, atom, wo, offs, out_0, out_1, 
             )
 
         sums_first = sb.tile([P, P], F32, name="sums_first")
-        sums_pair = picked[(last, PIECE)]
+        sums_pair = picked[(last, PIECE)][:, :P]
         sum_banks = [banks[4][:, :P], banks[0][:, :P], banks[0][:, P : 2 * P]]
-        backs = [banks[1][:, :G], banks[2][:, :G], banks[2][:, G : 2 * G]]
+        backs = [banks[1][:, :G], banks[2][:, :G]]
 
         def edge_sums(n, edges):
             for e in edges:
@@ -186,13 +186,13 @@ def tile_attend_filterconv_pl_kernel(tc, rad, wr, atom, wo, offs, out_0, out_1, 
                     op=ADD,
                 )
 
-        wo_bf = [area[:, start : start + HALF].bitcast(BF16) for start in pair_starts]
+        wo_first = sb.tile([P, PACK, 64 * PACK], BF16, name="wo_first", align_bytes=64)
+        wo_second = [area[:, start : start + PIECE].bitcast(BF16) for start in pair_starts]
 
-        def wo_views(u, lo, hi, walk):
-            h = lo // 64
-            dst = wo_bf[u].rearrange("p (t m j) -> p " + walk, t=2, j=PACK)
-            src = wo_raw[h][:].rearrange("p j (m u t) -> p u " + walk, u=2, t=2)[:, u]
-            return dst[:, lo:hi], src[:, lo - 64 * h : hi - 64 * h]
+        def second_views(u, lo, hi):
+            dst = wo_second[u].rearrange("p (t m j) -> p m j t", t=2, j=PACK)
+            src = wo_raw[1][:].rearrange("p j (m t) -> p m j t", t=PACK)[:, :, :, 2 * u : 2 * u + 2]
+            return dst[:, lo:hi], src[:, lo:hi]
 
         fused_product(last)
         for q in range(1, 4):
@@ -200,35 +200,47 @@ def tile_attend_filterconv_pl_kernel(tc, rad, wr, atom, wo, offs, out_0, out_1, 
         for q in range(1, 4):
             product(last, q * PIECE, (q + 1) * PIECE)
             last_sums(q - 1)
-        nc.scalar.copy(sums_pair, banks[0][:, : 2 * P])
-        for n in range(2):
-            nc.tensor.transpose(backs[1 + n], sums_pair[:, n * P : (n + 1) * P], ident[:])
-        for u in range(2):
-            nc.gpsimd.tensor_scalar(*wo_views(u, 0, 64, "m t j"), 1.0, 0.0, MULT, ADD)
+        nc.scalar.copy(
+            sums_pair.bitcast(BF16).rearrange("p (k t) -> p k t", t=2),
+            banks[0][:, : 2 * P].rearrange("p (t k) -> p k t", t=2),
+        )
+        nc.tensor.transpose(backs[1], sums_pair, ident[:])
+        nc.gpsimd.tensor_scalar(
+            wo_first[:].rearrange("p t (m j) -> p m t j", j=PACK),
+            wo_raw[0][:].rearrange("p j (m t) -> p m t j", t=PACK),
+            1.0,
+            0.0,
+            MULT,
+            ADD,
+        )
         last_sums(3)
-        nc.vector.tensor_copy(*wo_views(0, P - WO_LATE, P, "m j t"))
-        for u in range(2):
-            nc.scalar.copy(*wo_views(u, 64, P - WO_LATE, "m j t"))
-        nc.scalar.copy(b_bf[:, :, 0:2], banks[2][:, : 2 * G].rearrange("p (t g) -> p g t", t=2))
-        nc.scalar.copy(*wo_views(1, P - WO_LATE, P, "m j t"))
+        nc.scalar.copy(*second_views(1, 0, 64 - WO_LATE))
+        nc.vector.tensor_copy(*second_views(0, 0, 64))
+        nc.scalar.copy(b_bf[:, :, 0:2], backs[1].bitcast(BF16).rearrange("p (g t) -> p g t", t=2))
+        nc.scalar.copy(*second_views(1, 64 - WO_LATE, 64))
 
         wo_q = []
-
-        def quantise_wo(t):
+        for t in range(PACK):
             codes = sb.tile([P, P], U32, name="wo_codes%d" % t, align_bytes=64)
             scales = sb.tile([P, P], U8, name="wo_scales%d" % t, align_bytes=64)
-            nc.vector.quantize_mx(
-                out=codes[:].bitcast(FP8X4), scales=scales[:], in_=wo_bf[t // 2][:, t % 2 * P * PACK : (t % 2 + 1) * P * PACK]
-            )
             wo_q.append((codes, scales))
 
+        def quantise_wo(t, h):
+            codes, scales = wo_q[t]
+            source = wo_second[t // 2][:, t % 2 * PIECE : (t % 2 + 1) * PIECE] if h else wo_first[:, t, :]
+            cols = slice(64 * h, 64 * h + 64)
+            nc.vector.quantize_mx(out=codes[:, cols].bitcast(FP8X4), scales=scales[:, cols], in_=source)
+
+        quantise_wo(0, 0)
         b_codes = sb.tile([P, G], U32, name="b_codes", align_bytes=64)
         b_scales = sb.tile([P, G], U8, name="b_scales", align_bytes=64)
         nc.vector.quantize_mx(
             out=b_codes[:].bitcast(FP8X4), scales=b_scales[:], in_=b_bf[:].rearrange("p g t -> p (g t)")
         )
-        for t in range(PACK):
-            quantise_wo(t)
+        quantise_wo(0, 1)
+        for t in range(1, PACK):
+            for h in range(2):
+                quantise_wo(t, h)
         y = sb.tile([P, PACK, G], F32, name="y")
         for t in range(PACK):
             codes, scales = wo_q[t]

@@ -24,9 +24,6 @@ HALF = I // 2
 PIECE = I // 4
 WR_SPLIT = 88
 RAD_SPLIT = 344
-ORDER = (2, 0, 1, 3)
-BACK_AFTER = 2
-WO_LATE = 32
 
 
 def tile_attend_filterconv_pl_kernel(tc, rad, wr, atom, wo, offs, out_0, out_1, out_2):
@@ -47,14 +44,14 @@ def tile_attend_filterconv_pl_kernel(tc, rad, wr, atom, wo, offs, out_0, out_1, 
         nc.sync.dma_start(offsets[:], offs)
         atom_rows = atom.rearrange("(p t) n -> p t n", t=PACK)
         atoms = []
-        for t in ORDER:
+        for t in range(PACK):
             raw = sb.tile([P, T], F32, name="atom%d" % t, tag="atom%d" % t, align_bytes=64)
             nc.sync.dma_start(raw[:], atom_rows[:, t, :])
             atoms.append(raw)
         wo_rows = wo.rearrange("(p j) f -> p j f", j=PACK)
         wo_raw = []
         for h in range(2):
-            raw = sb.tile([P, PACK, F // 2], F32, name="wo_raw%d" % h)
+            raw = sb.tile([P, PACK, F // 2], F32, name="wo_raw%d" % h, tag="wo_raw%d" % h, align_bytes=64)
             nc.sync.dma_start(raw[:], wo_rows[:, :, h * F // 2 : (h + 1) * F // 2])
             wo_raw.append(raw)
 
@@ -87,124 +84,125 @@ def tile_attend_filterconv_pl_kernel(tc, rad, wr, atom, wo, offs, out_0, out_1, 
             rad_codes.append(codes)
             rad_scales.append(scales)
 
-        def filter_bank(n, h):
-            return banks[n] if h == 1 else banks[4 + n]
+        def filter_bank(t, h):
+            return banks[t] if h == 1 else banks[4 + t]
 
-        def filters(n, h):
-            cols = slice(ORDER[n] * P, (ORDER[n] + 1) * P)
-            nc.tensor.matmul_mx(
-                out=filter_bank(n, h)[:],
-                lhsT=wr_codes[:, cols].bitcast(FP8X4),
-                lhsT_scale=wr_scales[:, cols],
-                rhs=rad_codes[h][:].bitcast(FP8X4),
-                rhs_scale=rad_scales[h][:],
-                start=True,
-                stop=True,
-            )
+        for h in range(2):
+            for t in range(PACK):
+                cols = slice(t * P, (t + 1) * P)
+                nc.tensor.matmul_mx(
+                    out=filter_bank(t, h)[:],
+                    lhsT=wr_codes[:, cols].bitcast(FP8X4),
+                    lhsT_scale=wr_scales[:, cols],
+                    rhs=rad_codes[h][:].bitcast(FP8X4),
+                    rhs_scale=rad_scales[h][:],
+                    start=True,
+                    stop=True,
+                )
 
+        last = PACK - 1
         fused = [HALF, HALF, HALF, PIECE]
         third = sb.tile([P, I + HALF], F32, name="third", tag="rad_raw1")
         x = [area[:, 2 * I :], area[:, I : 2 * I], third[:, :I]]
         z = [third[:, :HALF], third[:, I:]]
-        last = PACK - 1
-        picked = {(n, HALF): x[n + 1][:, :HALF] for n in range(2)}
-        pair_starts = (0, HALF)
-        late_starts = [pair_starts[0] + P, pair_starts[1] + PIECE - 2 * WO_LATE]
-        picked[(last, PIECE)] = area[:, late_starts[1] : late_starts[1] + PIECE]
-        picked[(last, 2 * PIECE)] = x[0][:, :PIECE]
-        picked[(last, 3 * PIECE)] = area[:, late_starts[0] : late_starts[0] + PIECE]
+        picked = [x[1], x[2]]
 
-        def empty_filters(n):
-            nc.scalar.copy(z[n], filter_bank(n, 0)[:, : fused[n]])
+        def empty_filters(t):
+            nc.scalar.copy(z[t], filter_bank(t, 0)[:, : fused[t]])
 
-        def window(n, lo, hi):
-            return atoms[n][:].indirect(offsets[:, lo // 16 : hi // 16])
+        def window(t, lo, hi):
+            return atoms[t][:].indirect(offsets[:, lo // 16 : hi // 16])
 
-        def fused_product(n):
-            nc.vector.tensor_tensor(x[n][:, : fused[n]], window(n, 0, fused[n]), z[n], MULT)
+        def fused_product(t):
+            nc.vector.tensor_tensor(x[t][:, : fused[t]], window(t, 0, fused[t]), z[t], MULT)
 
-        def pick(n, lo, hi):
-            nc.scalar.activation(picked[(n, lo)], window(n, lo, hi), COPY)
+        def pick(t, q):
+            lo = q * PIECE
+            nc.scalar.activation(picked[t][:, lo - fused[t] : lo - fused[t] + PIECE], window(t, lo, lo + PIECE), COPY)
 
-        def product(n, lo, hi):
+        def product(t, q):
+            lo = q * PIECE
             h = lo // HALF
             nc.vector.tensor_tensor(
-                x[n][:, lo:hi], picked[(n, lo)], filter_bank(n, h)[:, lo - h * HALF : hi - h * HALF], MULT
+                x[t][:, lo : lo + PIECE],
+                picked[t][:, lo - fused[t] : lo - fused[t] + PIECE],
+                filter_bank(t, h)[:, lo - h * HALF : lo - h * HALF + PIECE],
+                MULT,
             )
 
-        sums_first = sb.tile([P, P], F32, name="sums_first")
-        sums_pair = picked[(last, PIECE)][:, :P]
-        sum_banks = [banks[4][:, :P], banks[0][:, :P], banks[0][:, P : 2 * P]]
-        backs = [banks[1][:, :G], banks[2][:, :G]]
-
-        def edge_sums(n, edges):
-            for e in edges:
+        def tensor_sums(t):
+            for e in range(EDGES):
                 nc.tensor.matmul(
-                    sum_banks[n],
-                    x[n][:, e:I:EDGES],
+                    banks[4][:, t * P : (t + 1) * P],
+                    x[t][:, e:I:EDGES],
                     ident[:],
                     start=(e == 0),
                     stop=(e == EDGES - 1),
                     is_transpose=True,
                 )
 
-        for h in range(2):
-            for n in range(PACK):
-                filters(n, h)
         empty_filters(0)
         empty_filters(1)
-        for n in range(last):
-            fused_product(n)
-            pick(n, HALF, I)
-            if n == 0:
-                third_filters = sb.tile([P, HALF], F32, name="third_filters", tag="atom%d" % ORDER[0], align_bytes=64)
+        for t in range(last):
+            fused_product(t)
+            for q in (2, 3):
+                pick(t, q)
+            if t == 0:
+                third_filters = sb.tile([P, HALF], F32, name="third_filters", tag="atom0", align_bytes=64)
                 z.append(third_filters[:])
                 empty_filters(2)
-            if n == 1:
-                fourth = sb.tile([P, I + PIECE], F32, name="fourth", tag="atom%d" % ORDER[1], align_bytes=64)
+            if t == 1:
+                fourth = sb.tile([P, I + 3 * P], F32, name="fourth", tag="atom1", align_bytes=64)
                 x.append(fourth[:, :I])
-                z.append(fourth[:, I:])
-                picked[(2, HALF)] = fourth[:, :HALF]
+                z.append(fourth[:, I : I + PIECE])
+                picked.append(fourth[:, :HALF])
                 empty_filters(3)
-            if n == 2:
-                b_bf = sb.tile([P, G, PACK], BF16, name="b_bf", tag="atom%d" % ORDER[0], align_bytes=64)
-                nc.scalar.copy(b_bf[:, :, 2:4], backs[0].unsqueeze(2).to_broadcast([P, G, 2]))
-            product(n, HALF, I)
-            edge_sums(n, range(BACK_AFTER))
-            if n == 1:
-                nc.tensor.transpose(backs[0], sums_first[:], ident[:])
-            edge_sums(n, range(BACK_AFTER, EDGES))
-            if n == 0:
-                nc.scalar.copy(sums_first[:], sum_banks[0])
+            for q in (2, 3):
+                product(t, q)
+            if t < 2:
+                tensor_sums(t)
+        picked.append(x[0])
+        b_bf = fourth[:, I + P :].bitcast(BF16).rearrange("p (g t) -> p g t", t=PACK)
 
-        def last_sums(q):
+        def vector_sums(t, first, source, terms):
+            view = source.rearrange("p (g e) -> p g e", e=terms)
             with nc.allow_low_precision(reason="float32 sum, rounded once to bfloat16 for the quantiser"):
                 nc.vector.tensor_reduce(
-                    out=b_bf[:, q * PIECE // EDGES : (q + 1) * PIECE // EDGES, ORDER[last]],
-                    in_=x[last][:, q * PIECE : (q + 1) * PIECE].rearrange("p (g e) -> p g e", e=EDGES),
-                    axis=mybir.AxisListType.X,
-                    op=ADD,
+                    out=b_bf[:, first : first + view.shape[1], t], in_=view, axis=mybir.AxisListType.X, op=ADD
                 )
 
-        wo_first = sb.tile([P, PACK, 64 * PACK], BF16, name="wo_first", align_bytes=64)
-        wo_second = [area[:, start : start + PIECE].bitcast(BF16) for start in pair_starts]
+        def piece_sums(t, q):
+            vector_sums(t, q * PIECE // EDGES, x[t][:, q * PIECE : (q + 1) * PIECE], EDGES)
 
-        def second_views(u, lo, hi):
-            dst = wo_second[u].rearrange("p (t m j) -> p m j t", t=2, j=PACK)
-            src = wo_raw[1][:].rearrange("p j (m t) -> p m j t", t=PACK)[:, :, :, 2 * u : 2 * u + 2]
-            return dst[:, lo:hi], src[:, lo:hi]
+        halves = sb.tile([P, PIECE], F32, name="halves")
+        by_edge = x[2][:, :HALF].rearrange("p (g e) -> p g e", e=EDGES)
+        nc.gpsimd.tensor_tensor(
+            halves[:].rearrange("p (g e) -> p g e", e=EDGES // 2),
+            by_edge[:, :, : EDGES // 2],
+            by_edge[:, :, EDGES // 2 :],
+            ADD,
+        )
+        for q in (2, 3):
+            piece_sums(2, q)
 
         fused_product(last)
-        for q in range(1, 4):
-            pick(last, q * PIECE, (q + 1) * PIECE)
-        for q in range(1, 4):
-            product(last, q * PIECE, (q + 1) * PIECE)
-            last_sums(q - 1)
+        sums_pair = z[last][:, :P]
+        pick(last, 1)
+        pick(last, 2)
         nc.scalar.copy(
             sums_pair.bitcast(BF16).rearrange("p (k t) -> p k t", t=2),
-            banks[0][:, : 2 * P].rearrange("p (t k) -> p k t", t=2),
+            banks[4][:, : 2 * P].rearrange("p (t k) -> p k t", t=2),
         )
-        nc.tensor.transpose(backs[1], sums_pair, ident[:])
+        nc.tensor.transpose(banks[5][:, :G], sums_pair, ident[:])
+        pick(last, 3)
+        nc.scalar.copy(b_bf[:, :, 0:2], banks[5][:, :G].bitcast(BF16).rearrange("p (g t) -> p g t", t=2))
+        vector_sums(2, 0, halves[:], EDGES // 2)
+        for q in range(1, 4):
+            product(last, q)
+            piece_sums(last, q - 1)
+        piece_sums(last, 3)
+
+        wo_first = sb.tile([P, PACK, 64 * PACK], BF16, name="wo_first", align_bytes=64)
         nc.gpsimd.tensor_scalar(
             wo_first[:].rearrange("p t (m j) -> p m t j", j=PACK),
             wo_raw[0][:].rearrange("p j (m t) -> p m t j", t=PACK),
@@ -213,41 +211,48 @@ def tile_attend_filterconv_pl_kernel(tc, rad, wr, atom, wo, offs, out_0, out_1, 
             MULT,
             ADD,
         )
-        last_sums(3)
-        nc.scalar.copy(*second_views(1, 0, 64 - WO_LATE))
-        nc.vector.tensor_copy(*second_views(0, 0, 64))
-        nc.scalar.copy(b_bf[:, :, 0:2], backs[1].bitcast(BF16).rearrange("p (g t) -> p g t", t=2))
-        nc.scalar.copy(*second_views(1, 64 - WO_LATE, 64))
+        wo_second = []
+        for u in range(2):
+            pair = sb.tile([P, 2, 64 * PACK], BF16, name="wo_second%d" % u, align_bytes=64)
+            nc.scalar.copy(
+                pair[:].rearrange("p t (m j) -> p m j t", j=PACK),
+                wo_raw[1][:].rearrange("p j (m t) -> p m j t", t=PACK)[:, :, :, 2 * u : 2 * u + 2],
+            )
+            wo_second.append(pair)
 
+        early_codes = sb.tile([P, 2, P], U32, name="early_codes", align_bytes=64)
+        late_codes = sb.tile([P, 2, P], U32, name="late_codes", tag="wo_raw1", align_bytes=64)
         wo_q = []
         for t in range(PACK):
-            codes = sb.tile([P, P], U32, name="wo_codes%d" % t, align_bytes=64)
+            codes = (early_codes, late_codes)[t // 2][:, t % 2, :]
             scales = sb.tile([P, P], U8, name="wo_scales%d" % t, align_bytes=64)
             wo_q.append((codes, scales))
 
         def quantise_wo(t, h):
             codes, scales = wo_q[t]
-            source = wo_second[t // 2][:, t % 2 * PIECE : (t % 2 + 1) * PIECE] if h else wo_first[:, t, :]
+            source = wo_second[t // 2][:, t % 2, :] if h else wo_first[:, t, :]
             cols = slice(64 * h, 64 * h + 64)
             nc.vector.quantize_mx(out=codes[:, cols].bitcast(FP8X4), scales=scales[:, cols], in_=source)
 
-        quantise_wo(0, 0)
-        b_codes = sb.tile([P, G], U32, name="b_codes", align_bytes=64)
+        for t in range(2):
+            quantise_wo(t, 0)
+        b_codes = sb.tile([P, G], U32, name="b_codes", tag="wo_raw0", align_bytes=64)
         b_scales = sb.tile([P, G], U8, name="b_scales", align_bytes=64)
         nc.vector.quantize_mx(
-            out=b_codes[:].bitcast(FP8X4), scales=b_scales[:], in_=b_bf[:].rearrange("p g t -> p (g t)")
+            out=b_codes[:].bitcast(FP8X4), scales=b_scales[:], in_=b_bf.rearrange("p g t -> p (g t)")
         )
-        quantise_wo(0, 1)
-        for t in range(1, PACK):
+        for t in range(2):
+            quantise_wo(t, 1)
+        for t in range(2, PACK):
             for h in range(2):
                 quantise_wo(t, h)
         y = sb.tile([P, PACK, G], F32, name="y")
         for t in range(PACK):
             codes, scales = wo_q[t]
-            bank = banks[(4, 5, 6, 1)[t]]
+            bank = banks[(0, 1, 2, 6)[t]]
             nc.tensor.matmul_mx(
                 out=bank[:, :G],
-                lhsT=codes[:].bitcast(FP8X4),
+                lhsT=codes.bitcast(FP8X4),
                 lhsT_scale=scales[:],
                 rhs=b_codes[:].bitcast(FP8X4),
                 rhs_scale=b_scales[:],

@@ -24,6 +24,7 @@ HALF = I // 2
 PIECE = I // 4
 WR_SPLIT = 88
 RAD_SPLIT = 344
+LAST_FUSED = 384
 
 
 def tile_attend_filterconv_pl_kernel(tc, rad, wr, atom, wo, offs, out_0, out_1, out_2):
@@ -101,7 +102,7 @@ def tile_attend_filterconv_pl_kernel(tc, rad, wr, atom, wo, offs, out_0, out_1, 
                 )
 
         last = PACK - 1
-        fused = [HALF, HALF, HALF, PIECE]
+        fused = [HALF, HALF, HALF, LAST_FUSED]
         third = sb.tile([P, I + HALF], F32, name="third", tag="rad_raw1")
         x = [area[:, 2 * I :], area[:, I : 2 * I], third[:, :I]]
         z = [third[:, :HALF], third[:, I:]]
@@ -113,20 +114,18 @@ def tile_attend_filterconv_pl_kernel(tc, rad, wr, atom, wo, offs, out_0, out_1, 
         def window(t, lo, hi):
             return atoms[t][:].indirect(offsets[:, lo // 16 : hi // 16])
 
-        def fused_product(t):
-            nc.vector.tensor_tensor(x[t][:, : fused[t]], window(t, 0, fused[t]), z[t], MULT)
+        def fused_product(t, lo, hi):
+            nc.vector.tensor_tensor(x[t][:, lo:hi], window(t, lo, hi), z[t][:, lo:hi], MULT)
 
-        def pick(t, q):
-            lo = q * PIECE
-            nc.scalar.activation(picked[t][:, lo - fused[t] : lo - fused[t] + PIECE], window(t, lo, lo + PIECE), COPY)
+        def pick(t, lo, hi):
+            nc.scalar.activation(picked[t][:, lo - fused[t] : hi - fused[t]], window(t, lo, hi), COPY)
 
-        def product(t, q):
-            lo = q * PIECE
+        def product(t, lo, hi):
             h = lo // HALF
             nc.vector.tensor_tensor(
-                x[t][:, lo : lo + PIECE],
-                picked[t][:, lo - fused[t] : lo - fused[t] + PIECE],
-                filter_bank(t, h)[:, lo - h * HALF : lo - h * HALF + PIECE],
+                x[t][:, lo:hi],
+                picked[t][:, lo - fused[t] : hi - fused[t]],
+                filter_bank(t, h)[:, lo - h * HALF : hi - h * HALF],
                 MULT,
             )
 
@@ -144,25 +143,25 @@ def tile_attend_filterconv_pl_kernel(tc, rad, wr, atom, wo, offs, out_0, out_1, 
         empty_filters(0)
         empty_filters(1)
         for t in range(last):
-            fused_product(t)
+            fused_product(t, 0, HALF)
             for q in (2, 3):
-                pick(t, q)
+                pick(t, q * PIECE, (q + 1) * PIECE)
             if t == 0:
                 third_filters = sb.tile([P, HALF], F32, name="third_filters", tag="atom0", align_bytes=64)
                 z.append(third_filters[:])
                 empty_filters(2)
             if t == 1:
-                fourth = sb.tile([P, I + 3 * P], F32, name="fourth", tag="atom1", align_bytes=64)
+                fourth = sb.tile([P, I + LAST_FUSED + P], F32, name="fourth", tag="atom1", align_bytes=64)
                 x.append(fourth[:, :I])
-                z.append(fourth[:, I : I + PIECE])
+                z.append(fourth[:, I : I + LAST_FUSED])
                 picked.append(fourth[:, :HALF])
                 empty_filters(3)
             for q in (2, 3):
-                product(t, q)
+                product(t, q * PIECE, (q + 1) * PIECE)
             if t < 2:
                 tensor_sums(t)
         picked.append(x[0])
-        b_bf = fourth[:, I + P :].bitcast(BF16).rearrange("p (g t) -> p g t", t=PACK)
+        b_bf = fourth[:, I + LAST_FUSED - P :].bitcast(BF16).rearrange("p (g t) -> p g t", t=PACK)
 
         def vector_sums(t, first, source, terms):
             view = source.rearrange("p (g e) -> p g e", e=terms)
@@ -171,8 +170,8 @@ def tile_attend_filterconv_pl_kernel(tc, rad, wr, atom, wo, offs, out_0, out_1, 
                     out=b_bf[:, first : first + view.shape[1], t], in_=view, axis=mybir.AxisListType.X, op=ADD
                 )
 
-        def piece_sums(t, q):
-            vector_sums(t, q * PIECE // EDGES, x[t][:, q * PIECE : (q + 1) * PIECE], EDGES)
+        def piece_sums(t, lo, hi):
+            vector_sums(t, lo // EDGES, x[t][:, lo:hi], EDGES)
 
         halves = sb.tile([P, PIECE], F32, name="halves")
         by_edge = x[2][:, :HALF].rearrange("p (g e) -> p g e", e=EDGES)
@@ -183,24 +182,26 @@ def tile_attend_filterconv_pl_kernel(tc, rad, wr, atom, wo, offs, out_0, out_1, 
             ADD,
         )
         for q in (2, 3):
-            piece_sums(2, q)
+            piece_sums(2, q * PIECE, (q + 1) * PIECE)
 
-        fused_product(last)
-        sums_pair = z[last][:, :P]
-        pick(last, 1)
-        pick(last, 2)
+        fused_product(last, LAST_FUSED - PIECE, LAST_FUSED)
+        fused_product(last, 0, LAST_FUSED - PIECE)
+        sums_pair = z[last][:, LAST_FUSED - PIECE : LAST_FUSED - P]
+        pick(last, LAST_FUSED, I - P)
         nc.scalar.copy(
             sums_pair.bitcast(BF16).rearrange("p (k t) -> p k t", t=2),
             banks[4][:, : 2 * P].rearrange("p (t k) -> p k t", t=2),
         )
         nc.tensor.transpose(banks[5][:, :G], sums_pair, ident[:])
-        pick(last, 3)
+        pick(last, I - P, I)
         nc.scalar.copy(b_bf[:, :, 0:2], banks[5][:, :G].bitcast(BF16).rearrange("p (g t) -> p g t", t=2))
         vector_sums(2, 0, halves[:], EDGES // 2)
-        for q in range(1, 4):
-            product(last, q)
-            piece_sums(last, q - 1)
-        piece_sums(last, 3)
+        piece_sums(last, 0, LAST_FUSED)
+        product(last, LAST_FUSED, HALF)
+        product(last, HALF, I - P)
+        product(last, I - P, I)
+        piece_sums(last, LAST_FUSED, I - P)
+        piece_sums(last, I - P, I)
 
         wo_first = sb.tile([P, PACK, 64 * PACK], BF16, name="wo_first", align_bytes=64)
         nc.gpsimd.tensor_scalar(

@@ -24,7 +24,8 @@ HALF = I // 2
 PIECE = I // 4
 WR_SPLIT = 88
 RAD_SPLIT = 344
-LAST_FUSED = 384
+LAST_FUSED = 256
+WO_VECTOR = 16
 
 
 def tile_attend_filterconv_pl_kernel(tc, rad, wr, atom, wo, offs, out_0, out_1, out_2):
@@ -161,6 +162,12 @@ def tile_attend_filterconv_pl_kernel(tc, rad, wr, atom, wo, offs, out_0, out_1, 
             if t < 2:
                 tensor_sums(t)
         picked.append(x[0])
+        sums_pair = sb.tile([P, P], F32, name="sums_pair", tag="atom2", align_bytes=64)
+        nc.scalar.copy(
+            sums_pair[:].bitcast(BF16).rearrange("p (k t) -> p k t", t=2),
+            banks[4][:, : 2 * P].rearrange("p (t k) -> p k t", t=2),
+        )
+        nc.tensor.transpose(banks[5][:, :G], sums_pair[:], ident[:])
         b_bf = fourth[:, I + LAST_FUSED - P :].bitcast(BF16).rearrange("p (g t) -> p g t", t=PACK)
 
         def vector_sums(t, first, source, terms):
@@ -184,24 +191,21 @@ def tile_attend_filterconv_pl_kernel(tc, rad, wr, atom, wo, offs, out_0, out_1, 
         for q in (2, 3):
             piece_sums(2, q * PIECE, (q + 1) * PIECE)
 
-        fused_product(last, LAST_FUSED - PIECE, LAST_FUSED)
-        fused_product(last, 0, LAST_FUSED - PIECE)
-        sums_pair = z[last][:, LAST_FUSED - PIECE : LAST_FUSED - P]
-        pick(last, LAST_FUSED, I - P)
-        nc.scalar.copy(
-            sums_pair.bitcast(BF16).rearrange("p (k t) -> p k t", t=2),
-            banks[4][:, : 2 * P].rearrange("p (t k) -> p k t", t=2),
-        )
-        nc.tensor.transpose(banks[5][:, :G], sums_pair, ident[:])
-        pick(last, I - P, I)
+        fused_product(last, LAST_FUSED - P, LAST_FUSED)
+        fused_product(last, 0, LAST_FUSED - P)
+        cuts = (LAST_FUSED, HALF + P, I - P, I)
+        for lo, hi in zip(cuts, cuts[1:]):
+            pick(last, lo, hi)
         nc.scalar.copy(b_bf[:, :, 0:2], banks[5][:, :G].bitcast(BF16).rearrange("p (g t) -> p g t", t=2))
         vector_sums(2, 0, halves[:], EDGES // 2)
         piece_sums(last, 0, LAST_FUSED)
         product(last, LAST_FUSED, HALF)
-        product(last, HALF, I - P)
-        product(last, I - P, I)
-        piece_sums(last, LAST_FUSED, I - P)
-        piece_sums(last, I - P, I)
+        product(last, HALF, cuts[1])
+        product(last, cuts[1], cuts[2])
+        piece_sums(last, cuts[0], cuts[1])
+        product(last, cuts[2], I)
+        piece_sums(last, cuts[1], cuts[2])
+        piece_sums(last, cuts[2], I)
 
         wo_first = sb.tile([P, PACK, 64 * PACK], BF16, name="wo_first", align_bytes=64)
         nc.gpsimd.tensor_scalar(
@@ -215,10 +219,12 @@ def tile_attend_filterconv_pl_kernel(tc, rad, wr, atom, wo, offs, out_0, out_1, 
         wo_second = []
         for u in range(2):
             pair = sb.tile([P, 2, 64 * PACK], BF16, name="wo_second%d" % u, align_bytes=64)
-            nc.scalar.copy(
-                pair[:].rearrange("p t (m j) -> p m j t", j=PACK),
-                wo_raw[1][:].rearrange("p j (m t) -> p m j t", t=PACK)[:, :, :, 2 * u : 2 * u + 2],
-            )
+            dst = pair[:].rearrange("p t (m j) -> p m j t", j=PACK)
+            src = wo_raw[1][:].rearrange("p j (m t) -> p m j t", t=PACK)[:, :, :, 2 * u : 2 * u + 2]
+            split = WO_VECTOR * u
+            nc.scalar.copy(dst[:, split:], src[:, split:])
+            if split:
+                nc.vector.tensor_copy(dst[:, :split], src[:, :split])
             wo_second.append(pair)
 
         early_codes = sb.tile([P, 2, P], U32, name="early_codes", align_bytes=64)

@@ -25,7 +25,7 @@ PIECE = I // 4
 WR_SPLIT = 88
 RAD_SPLIT = 344
 LAST_FUSED = 256
-WO_VECTOR = 16
+WO_VECTOR = 32
 
 
 def tile_attend_filterconv_pl_kernel(tc, rad, wr, atom, wo, offs, out_0, out_1, out_2):
@@ -266,7 +266,10 @@ def tile_attend_filterconv_pl_kernel(tc, rad, wr, atom, wo, offs, out_0, out_1, 
                 start=True,
                 stop=True,
             )
-            nc.scalar.copy(y[:, t, :], bank[:, :G])
+            pieces = 2 if t == last else 1
+            for h in range(pieces):
+                cols = slice(h * G // pieces, (h + 1) * G // pieces)
+                nc.scalar.copy(y[:, t, cols], bank[:, cols])
         nc.sync.dma_start(out_0.rearrange("(p t) g -> p t g", t=PACK), y[:])
 
         y_bf = sb.tile([P, G * PACK], BF16, name="y_bf", align_bytes=64)

@@ -22,8 +22,8 @@ PACK = 4
 EDGES = I // G
 HALF = I // 2
 PIECE = I // 4
-WR_SPLIT = 88
-RAD_SPLIT = 344
+WR_VECTOR = (96, 64)
+RAD_VECTOR = 640
 LAST_FUSED = 256
 WO_VECTOR = 32
 
@@ -35,19 +35,19 @@ def tile_attend_filterconv_pl_kernel(tc, rad, wr, atom, wo, offs, out_0, out_1, 
         ps = ctx.enter_context(tc.psum_pool(name="ps", bufs=1))
 
         offsets = sb.tile([P, I // 16], U16, name="offsets")
-        wr_raw = sb.tile([P, PACK, K], F32, name="wr_raw")
-        nc.sync.dma_start(wr_raw[:], wr.rearrange("(p j) k -> p j k", j=PACK))
-        rad_rows = rad.rearrange("(p j) i -> p j i", j=PACK)
+        rad_rows = rad.rearrange("(p u e) i -> p u e i", u=2, e=2)
         rad_raw = []
-        for h in range(2):
-            raw = sb.tile([P, PACK, HALF], F32, name="rad_raw%d" % h, tag="rad_raw%d" % h)
-            nc.sync.dma_start(raw[:], rad_rows[:, :, h * HALF : (h + 1) * HALF])
+        for u in range(2):
+            raw = sb.tile([P, 2, I], F32, name="rad_raw%d" % u, tag="rad_raw%d" % u, align_bytes=256)
+            nc.sync.dma_start(raw[:], rad_rows[:, u, :, :])
             rad_raw.append(raw)
+        wr_raw = sb.tile([P, PACK, K], F32, name="wr_raw", align_bytes=256)
+        nc.sync.dma_start(wr_raw[:], wr.rearrange("(p j) k -> p j k", j=PACK))
         nc.sync.dma_start(offsets[:], offs)
         atom_rows = atom.rearrange("(p t) n -> p t n", t=PACK)
         atoms = []
         for t in range(PACK):
-            raw = sb.tile([P, T], F32, name="atom%d" % t, tag="atom%d" % t, align_bytes=64)
+            raw = sb.tile([P, T], F32, name="atom%d" % t, tag="atom%d" % t, align_bytes=256)
             nc.sync.dma_start(raw[:], atom_rows[:, t, :])
             atoms.append(raw)
         wo_rows = wo.rearrange("(p j) f -> p j f", j=PACK)
@@ -62,55 +62,81 @@ def tile_attend_filterconv_pl_kernel(tc, rad, wr, atom, wo, offs, out_0, out_1, 
 
         banks = [ps.tile([P, HALF], F32, name="bank%d" % n) for n in range(8)]
 
-        wr_bf = sb.tile([P, K * PACK], BF16, name="wr_bf", align_bytes=64)
-        wr_dst = wr_bf[:].rearrange("p (t m j) -> p m t j", t=PACK, j=PACK)
-        wr_src = wr_raw[:].rearrange("p j (m t) -> p m t j", t=PACK)
-        nc.vector.tensor_copy(wr_dst[:, :WR_SPLIT, :, :], wr_src[:, :WR_SPLIT, :, :])
-        nc.scalar.copy(wr_dst[:, WR_SPLIT:, :, :], wr_src[:, WR_SPLIT:, :, :])
-        wr_codes = sb.tile([P, K], U32, name="wr_codes", align_bytes=64)
-        wr_scales = sb.tile([P, K], U8, name="wr_scales", align_bytes=64)
-        nc.vector.quantize_mx(out=wr_codes[:].bitcast(FP8X4), scales=wr_scales[:], in_=wr_bf[:])
+        rad_bf = [sb.tile([P, HALF * PACK], BF16, name="rad_bf%d" % h, align_bytes=64) for h in range(2)]
 
-        area = sb.tile([P, 3 * I], F32, name="area", align_bytes=64)
-        rad_first = sb.tile([P, HALF * PACK], BF16, name="rad_first", align_bytes=64)
-        rad_bf = [rad_first[:], area[:, I + PIECE : 2 * I + PIECE].bitcast(BF16)]
+        def round_rad(copy, u, lo, hi):
+            h = lo // HALF
+            dst = rad_bf[h][:].rearrange("p (c i j) -> p c j i", i=4, j=PACK)[:, :, 2 * u : 2 * u + 2, :]
+            src = rad_raw[u][:, :, lo:hi].rearrange("p e (c i) -> p c e i", i=4)
+            copy(dst[:, (lo - h * HALF) // 4 : (hi - h * HALF) // 4], src)
+
+        for u in range(2):
+            round_rad(nc.vector.tensor_copy, u, 0, HALF)
+            round_rad(nc.vector.tensor_copy, u, HALF, RAD_VECTOR)
+            round_rad(nc.scalar.copy, u, RAD_VECTOR, I)
         rad_codes, rad_scales = [], []
         for h in range(2):
-            dst = rad_bf[h].rearrange("p (c i j) -> p c j i", i=4, j=PACK)
-            src = rad_raw[h][:].rearrange("p j (c i) -> p c j i", i=4)
-            nc.vector.tensor_copy(dst[:, : RAD_SPLIT // 4, :, :], src[:, : RAD_SPLIT // 4, :, :])
-            nc.scalar.copy(dst[:, RAD_SPLIT // 4 :, :, :], src[:, RAD_SPLIT // 4 :, :, :])
             codes = sb.tile([P, HALF], U32, name="rad_codes%d" % h, align_bytes=64)
             scales = sb.tile([P, HALF], U8, name="rad_scales%d" % h, align_bytes=64)
-            nc.vector.quantize_mx(out=codes[:].bitcast(FP8X4), scales=scales[:], in_=rad_bf[h])
+            nc.vector.quantize_mx(out=codes[:].bitcast(FP8X4), scales=scales[:], in_=rad_bf[h][:])
             rad_codes.append(codes)
             rad_scales.append(scales)
 
-        def filter_bank(t, h):
-            return banks[t] if h == 1 else banks[4 + t]
-
-        for h in range(2):
-            for t in range(PACK):
-                cols = slice(t * P, (t + 1) * P)
-                nc.tensor.matmul_mx(
-                    out=filter_bank(t, h)[:],
-                    lhsT=wr_codes[:, cols].bitcast(FP8X4),
-                    lhsT_scale=wr_scales[:, cols],
-                    rhs=rad_codes[h][:].bitcast(FP8X4),
-                    rhs_scale=rad_scales[h][:],
-                    start=True,
-                    stop=True,
-                )
+        wr_q = []
+        for u in range(2):
+            pair = sb.tile([P, 2, P * PACK], BF16, name="wr_bf%d" % u, align_bytes=64)
+            dst = pair[:].rearrange("p t (m j) -> p m j t", j=PACK)
+            src = wr_raw[:].rearrange("p j (m t) -> p m j t", t=PACK)[:, :, :, 2 * u : 2 * u + 2]
+            split = WR_VECTOR[u]
+            nc.vector.tensor_copy(dst[:, :split], src[:, :split])
+            nc.scalar.copy(dst[:, split:], src[:, split:])
+            for e in range(2):
+                codes = sb.tile([P, P], U32, name="wr_codes%d" % (2 * u + e), align_bytes=64)
+                scales = sb.tile([P, P], U8, name="wr_scales%d" % (2 * u + e), align_bytes=64)
+                nc.vector.quantize_mx(out=codes[:].bitcast(FP8X4), scales=scales[:], in_=pair[:, e, :])
+                wr_q.append((codes, scales))
 
         last = PACK - 1
+        places = [
+            [(0, 0), (1, 0), (2, 0), (2, PIECE)],
+            [(3, 0), (3, PIECE), (4, 0), (4, PIECE)],
+            [(5, 0), (5, PIECE), (6, 0), (6, PIECE)],
+            [(7, 0), (0, PIECE), (4, 0), (4, PIECE)],
+        ]
+
+        def filters(t, lo, hi):
+            bank, first = places[t][lo // PIECE]
+            start = first + lo % PIECE
+            return banks[bank][:, start : start + hi - lo]
+
+        def make_filters(t, lo, hi):
+            h = lo // HALF
+            cols = slice(lo - h * HALF, hi - h * HALF)
+            nc.tensor.matmul_mx(
+                out=filters(t, lo, hi),
+                lhsT=wr_q[t][0][:].bitcast(FP8X4),
+                lhsT_scale=wr_q[t][1][:],
+                rhs=rad_codes[h][:, cols].bitcast(FP8X4),
+                rhs_scale=rad_scales[h][:, cols],
+                start=True,
+                stop=True,
+            )
+
+        make_filters(0, 0, PIECE)
+        make_filters(0, PIECE, HALF)
+        make_filters(0, HALF, I)
+        for t in (1, 2):
+            make_filters(t, 0, HALF)
+            make_filters(t, HALF, I)
+        make_filters(last, 0, PIECE)
+
         fused = [HALF, HALF, HALF, LAST_FUSED]
-        third = sb.tile([P, I + HALF], F32, name="third", tag="rad_raw1")
-        x = [area[:, 2 * I :], area[:, I : 2 * I], third[:, :I]]
-        z = [third[:, :HALF], third[:, I:]]
+        x = [sb.tile([P, I], F32, name="x%d" % t)[:] for t in range(last)]
+        z = [sb.tile([P, HALF], F32, name="z")[:]] * last
         picked = [x[1], x[2]]
 
-        def empty_filters(t):
-            nc.scalar.copy(z[t], filter_bank(t, 0)[:, : fused[t]])
+        def empty_filters(t, lo, hi):
+            nc.scalar.copy(z[t][:, lo:hi], filters(t, lo, hi))
 
         def window(t, lo, hi):
             return atoms[t][:].indirect(offsets[:, lo // 16 : hi // 16])
@@ -122,18 +148,14 @@ def tile_attend_filterconv_pl_kernel(tc, rad, wr, atom, wo, offs, out_0, out_1, 
             nc.scalar.activation(picked[t][:, lo - fused[t] : hi - fused[t]], window(t, lo, hi), COPY)
 
         def product(t, lo, hi):
-            h = lo // HALF
             nc.vector.tensor_tensor(
-                x[t][:, lo:hi],
-                picked[t][:, lo - fused[t] : hi - fused[t]],
-                filter_bank(t, h)[:, lo - h * HALF : hi - h * HALF],
-                MULT,
+                x[t][:, lo:hi], picked[t][:, lo - fused[t] : hi - fused[t]], filters(t, lo, hi), MULT
             )
 
         def tensor_sums(t):
             for e in range(EDGES):
                 nc.tensor.matmul(
-                    banks[4][:, t * P : (t + 1) * P],
+                    banks[0][:, t * P : (t + 1) * P],
                     x[t][:, e:I:EDGES],
                     ident[:],
                     start=(e == 0),
@@ -141,34 +163,37 @@ def tile_attend_filterconv_pl_kernel(tc, rad, wr, atom, wo, offs, out_0, out_1, 
                     is_transpose=True,
                 )
 
-        empty_filters(0)
-        empty_filters(1)
+        for q in range(2):
+            empty_filters(0, q * PIECE, (q + 1) * PIECE)
         for t in range(last):
-            fused_product(t, 0, HALF)
+            for q in range(2):
+                fused_product(t, q * PIECE, (q + 1) * PIECE)
             for q in (2, 3):
                 pick(t, q * PIECE, (q + 1) * PIECE)
-            if t == 0:
-                third_filters = sb.tile([P, HALF], F32, name="third_filters", tag="atom0", align_bytes=64)
-                z.append(third_filters[:])
-                empty_filters(2)
+            if t < 2:
+                for q in range(2):
+                    empty_filters(t + 1, q * PIECE, (q + 1) * PIECE)
             if t == 1:
-                fourth = sb.tile([P, I + LAST_FUSED + P], F32, name="fourth", tag="atom1", align_bytes=64)
+                fourth = sb.tile([P, I + LAST_FUSED + P], F32, name="fourth", tag="atom1", align_bytes=256)
                 x.append(fourth[:, :I])
                 z.append(fourth[:, I : I + LAST_FUSED])
                 picked.append(fourth[:, :HALF])
-                empty_filters(3)
+                empty_filters(3, 0, LAST_FUSED)
             for q in (2, 3):
                 product(t, q * PIECE, (q + 1) * PIECE)
             if t < 2:
                 tensor_sums(t)
+            if t == 1:
+                make_filters(last, HALF, I)
         picked.append(x[0])
-        sums_pair = sb.tile([P, P], F32, name="sums_pair", tag="atom2", align_bytes=64)
+        sums_pair = sb.tile([P, P], F32, name="sums_pair", tag="atom2", align_bytes=256)
         nc.scalar.copy(
             sums_pair[:].bitcast(BF16).rearrange("p (k t) -> p k t", t=2),
-            banks[4][:, : 2 * P].rearrange("p (t k) -> p k t", t=2),
+            banks[0][:, : 2 * P].rearrange("p (t k) -> p k t", t=2),
         )
-        nc.tensor.transpose(banks[5][:, :G], sums_pair[:], ident[:])
-        b_bf = fourth[:, I + LAST_FUSED - P :].bitcast(BF16).rearrange("p (g t) -> p g t", t=PACK)
+        nc.tensor.transpose(banks[1][:, :G], sums_pair[:], ident[:])
+        make_filters(last, PIECE, HALF)
+        b_bf = fourth[:, I + LAST_FUSED - P : I + LAST_FUSED + P].bitcast(BF16).rearrange("p (g t) -> p g t", t=PACK)
 
         def vector_sums(t, first, source, terms):
             view = source.rearrange("p (g e) -> p g e", e=terms)
@@ -196,7 +221,7 @@ def tile_attend_filterconv_pl_kernel(tc, rad, wr, atom, wo, offs, out_0, out_1, 
         cuts = (LAST_FUSED, HALF + P, I - P, I)
         for lo, hi in zip(cuts, cuts[1:]):
             pick(last, lo, hi)
-        nc.scalar.copy(b_bf[:, :, 0:2], banks[5][:, :G].bitcast(BF16).rearrange("p (g t) -> p g t", t=2))
+        nc.scalar.copy(b_bf[:, :, 0:2], banks[1][:, :G].bitcast(BF16).rearrange("p (g t) -> p g t", t=2))
         vector_sums(2, 0, halves[:], EDGES // 2)
         piece_sums(last, 0, LAST_FUSED)
         product(last, LAST_FUSED, HALF)
@@ -256,7 +281,7 @@ def tile_attend_filterconv_pl_kernel(tc, rad, wr, atom, wo, offs, out_0, out_1, 
         y = sb.tile([P, PACK, G], F32, name="y")
         for t in range(PACK):
             codes, scales = wo_q[t]
-            bank = banks[(0, 1, 2, 6)[t]]
+            bank = banks[(2, 3, 5, 6)[t]]
             nc.tensor.matmul_mx(
                 out=bank[:, :G],
                 lhsT=codes.bitcast(FP8X4),

@@ -25,6 +25,7 @@ PIECE = I // 4
 WR_VECTOR = (96, 64)
 RAD_VECTOR = 640
 LAST_FUSED = 256
+LEAD = 64
 WO_VECTOR = 32
 
 
@@ -101,7 +102,7 @@ def tile_attend_filterconv_pl_kernel(tc, rad, wr, atom, wo, offs, out_0, out_1, 
             [(0, 0), (1, 0), (2, 0), (2, PIECE)],
             [(3, 0), (3, PIECE), (4, 0), (4, PIECE)],
             [(5, 0), (5, PIECE), (6, 0), (6, PIECE)],
-            [(7, 0), (0, PIECE), (4, 0), (4, PIECE)],
+            [(7, 0), (7, PIECE), (4, 0), (4, PIECE)],
         ]
 
         def filters(t, lo, hi):
@@ -128,7 +129,7 @@ def tile_attend_filterconv_pl_kernel(tc, rad, wr, atom, wo, offs, out_0, out_1, 
         for t in (1, 2):
             make_filters(t, 0, HALF)
             make_filters(t, HALF, I)
-        make_filters(last, 0, PIECE)
+        make_filters(last, 0, HALF)
 
         fused = [HALF, HALF, HALF, LAST_FUSED]
         x = [sb.tile([P, I], F32, name="x%d" % t)[:] for t in range(last)]
@@ -174,11 +175,14 @@ def tile_attend_filterconv_pl_kernel(tc, rad, wr, atom, wo, offs, out_0, out_1, 
                 for q in range(2):
                     empty_filters(t + 1, q * PIECE, (q + 1) * PIECE)
             if t == 1:
-                fourth = sb.tile([P, I + LAST_FUSED + P], F32, name="fourth", tag="atom1", align_bytes=256)
+                fourth = sb.tile([P, I + LAST_FUSED + 3 * P], F32, name="fourth", tag="atom1", align_bytes=256)
                 x.append(fourth[:, :I])
                 z.append(fourth[:, I : I + LAST_FUSED])
                 picked.append(fourth[:, :HALF])
-                empty_filters(3, 0, LAST_FUSED)
+                empty_filters(3, 0, LAST_FUSED - LEAD)
+                shared = I + LAST_FUSED + P
+                lead_filters = fourth[:, shared - LEAD // 2 : shared + LEAD // 2]
+                nc.scalar.copy(lead_filters, filters(last, LAST_FUSED - LEAD, LAST_FUSED))
             for q in (2, 3):
                 product(t, q * PIECE, (q + 1) * PIECE)
             if t < 2:
@@ -186,14 +190,8 @@ def tile_attend_filterconv_pl_kernel(tc, rad, wr, atom, wo, offs, out_0, out_1, 
             if t == 1:
                 make_filters(last, HALF, I)
         picked.append(x[0])
-        sums_pair = sb.tile([P, P], F32, name="sums_pair", tag="atom2", align_bytes=256)
-        nc.scalar.copy(
-            sums_pair[:].bitcast(BF16).rearrange("p (k t) -> p k t", t=2),
-            banks[0][:, : 2 * P].rearrange("p (t k) -> p k t", t=2),
-        )
-        nc.tensor.transpose(banks[1][:, :G], sums_pair[:], ident[:])
-        make_filters(last, PIECE, HALF)
-        b_bf = fourth[:, I + LAST_FUSED - P : I + LAST_FUSED + P].bitcast(BF16).rearrange("p (g t) -> p g t", t=PACK)
+        sums_pair = fourth[:, shared - P : shared]
+        b_bf = fourth[:, shared:].bitcast(BF16).rearrange("p (g t) -> p g t", t=PACK)
 
         def vector_sums(t, first, source, terms):
             view = source.rearrange("p (g e) -> p g e", e=terms)
@@ -216,21 +214,30 @@ def tile_attend_filterconv_pl_kernel(tc, rad, wr, atom, wo, offs, out_0, out_1, 
         for q in (2, 3):
             piece_sums(2, q * PIECE, (q + 1) * PIECE)
 
-        fused_product(last, LAST_FUSED - P, LAST_FUSED)
-        fused_product(last, 0, LAST_FUSED - P)
-        cuts = (LAST_FUSED, HALF + P, I - P, I)
-        for lo, hi in zip(cuts, cuts[1:]):
+        lo, hi = LAST_FUSED - LEAD, LAST_FUSED
+        nc.vector.tensor_tensor(x[last][:, lo:hi], window(last, lo, hi), lead_filters, MULT)
+        fused_product(last, 0, lo)
+        cuts = (LAST_FUSED, HALF, HALF + P, I - P, I)
+        for lo, hi in zip(cuts[:2], cuts[1:3]):
+            pick(last, lo, hi)
+        nc.scalar.copy(
+            sums_pair.bitcast(BF16).rearrange("p (k t) -> p k t", t=2),
+            banks[0][:, : 2 * P].rearrange("p (t k) -> p k t", t=2),
+        )
+        nc.tensor.transpose(banks[1][:, :G], sums_pair, ident[:])
+        for lo, hi in zip(cuts[2:], cuts[3:]):
             pick(last, lo, hi)
         nc.scalar.copy(b_bf[:, :, 0:2], banks[1][:, :G].bitcast(BF16).rearrange("p (g t) -> p g t", t=2))
         vector_sums(2, 0, halves[:], EDGES // 2)
-        piece_sums(last, 0, LAST_FUSED)
-        product(last, LAST_FUSED, HALF)
-        product(last, HALF, cuts[1])
+        product(last, cuts[0], cuts[1])
         product(last, cuts[1], cuts[2])
+        piece_sums(last, 0, cuts[0])
         piece_sums(last, cuts[0], cuts[1])
-        product(last, cuts[2], I)
+        product(last, cuts[2], cuts[3])
         piece_sums(last, cuts[1], cuts[2])
-        piece_sums(last, cuts[2], I)
+        product(last, cuts[3], I)
+        piece_sums(last, cuts[2], cuts[3])
+        piece_sums(last, cuts[3], I)
 
         wo_first = sb.tile([P, PACK, 64 * PACK], BF16, name="wo_first", align_bytes=64)
         nc.gpsimd.tensor_scalar(

@@ -35,7 +35,7 @@ def tile_attend_filterconv_pl_kernel(tc, rad, wr, atom, wo, offs, out_0, out_1, 
         sb = ctx.enter_context(tc.tile_pool(name="sb", bufs=1))
         ps = ctx.enter_context(tc.psum_pool(name="ps", bufs=1))
 
-        offsets = sb.tile([P, I // 16], U16, name="offsets")
+        offsets = sb.tile([P, I // 16], U16, name="offsets", align_bytes=256)
         rad_rows = rad.rearrange("(p u e) i -> p u e i", u=2, e=2)
         rad_raw = []
         for u in range(2):
@@ -54,7 +54,7 @@ def tile_attend_filterconv_pl_kernel(tc, rad, wr, atom, wo, offs, out_0, out_1, 
         wo_rows = wo.rearrange("(p j) f -> p j f", j=PACK)
         wo_raw = []
         for h in range(2):
-            raw = sb.tile([P, PACK, F // 2], F32, name="wo_raw%d" % h, tag="wo_raw%d" % h, align_bytes=64)
+            raw = sb.tile([P, PACK, F // 2], F32, name="wo_raw%d" % h, tag="wo_raw%d" % h, align_bytes=256)
             nc.sync.dma_start(raw[:], wo_rows[:, :, h * F // 2 : (h + 1) * F // 2])
             wo_raw.append(raw)
 
@@ -132,9 +132,9 @@ def tile_attend_filterconv_pl_kernel(tc, rad, wr, atom, wo, offs, out_0, out_1, 
         make_filters(last, 0, HALF)
 
         fused = [HALF, HALF, HALF, LAST_FUSED]
-        x = [sb.tile([P, I], F32, name="x%d" % t)[:] for t in range(last)]
+        x = [sb.tile([P, I], F32, name="x%d" % t)[:] for t in range(PACK)]
         z = [sb.tile([P, HALF], F32, name="z")[:]] * last
-        picked = [x[1], x[2]]
+        picked = [x[1], x[2], x[3], x[0]]
 
         def empty_filters(t, lo, hi):
             nc.scalar.copy(z[t][:, lo:hi], filters(t, lo, hi))
@@ -164,8 +164,8 @@ def tile_attend_filterconv_pl_kernel(tc, rad, wr, atom, wo, offs, out_0, out_1, 
                     is_transpose=True,
                 )
 
-        for q in range(2):
-            empty_filters(0, q * PIECE, (q + 1) * PIECE)
+        empty_filters(0, 0, PIECE)
+        nc.vector.tensor_copy(z[0][:, PIECE:HALF], filters(0, PIECE, HALF))
         for t in range(last):
             for q in range(2):
                 fused_product(t, q * PIECE, (q + 1) * PIECE)
@@ -174,13 +174,11 @@ def tile_attend_filterconv_pl_kernel(tc, rad, wr, atom, wo, offs, out_0, out_1, 
             if t < 2:
                 for q in range(2):
                     empty_filters(t + 1, q * PIECE, (q + 1) * PIECE)
-            if t == 1:
-                fourth = sb.tile([P, I + LAST_FUSED + 3 * P], F32, name="fourth", tag="atom1", align_bytes=256)
-                x.append(fourth[:, :I])
-                z.append(fourth[:, I : I + LAST_FUSED])
-                picked.append(fourth[:, :HALF])
+            if t == 2:
+                fourth = sb.tile([P, LAST_FUSED + 3 * P], F32, name="fourth", tag="atom2", align_bytes=256)
+                z.append(fourth[:, :LAST_FUSED])
                 empty_filters(3, 0, LAST_FUSED - LEAD)
-                shared = I + LAST_FUSED + P
+                shared = LAST_FUSED + P
                 lead_filters = fourth[:, shared - LEAD // 2 : shared + LEAD // 2]
                 nc.scalar.copy(lead_filters, filters(last, LAST_FUSED - LEAD, LAST_FUSED))
             for q in (2, 3):
@@ -189,7 +187,6 @@ def tile_attend_filterconv_pl_kernel(tc, rad, wr, atom, wo, offs, out_0, out_1, 
                 tensor_sums(t)
             if t == 1:
                 make_filters(last, HALF, I)
-        picked.append(x[0])
         sums_pair = fourth[:, shared - P : shared]
         b_bf = fourth[:, shared:].bitcast(BF16).rearrange("p (g t) -> p g t", t=PACK)
 
@@ -260,7 +257,7 @@ def tile_attend_filterconv_pl_kernel(tc, rad, wr, atom, wo, offs, out_0, out_1, 
             wo_second.append(pair)
 
         early_codes = sb.tile([P, 2, P], U32, name="early_codes", align_bytes=64)
-        late_codes = sb.tile([P, 2, P], U32, name="late_codes", tag="wo_raw1", align_bytes=64)
+        late_codes = sb.tile([P, 2, P], U32, name="late_codes", tag="wo_raw1", align_bytes=256)
         wo_q = []
         for t in range(PACK):
             codes = (early_codes, late_codes)[t // 2][:, t % 2, :]
@@ -275,7 +272,7 @@ def tile_attend_filterconv_pl_kernel(tc, rad, wr, atom, wo, offs, out_0, out_1, 
 
         for t in range(2):
             quantise_wo(t, 0)
-        b_codes = sb.tile([P, G], U32, name="b_codes", tag="wo_raw0", align_bytes=64)
+        b_codes = sb.tile([P, G], U32, name="b_codes", tag="wo_raw0", align_bytes=256)
         b_scales = sb.tile([P, G], U8, name="b_scales", align_bytes=64)
         nc.vector.quantize_mx(
             out=b_codes[:].bitcast(FP8X4), scales=b_scales[:], in_=b_bf.rearrange("p g t -> p (g t)")
@@ -285,7 +282,7 @@ def tile_attend_filterconv_pl_kernel(tc, rad, wr, atom, wo, offs, out_0, out_1, 
         for t in range(2, PACK):
             for h in range(2):
                 quantise_wo(t, h)
-        y = sb.tile([P, PACK, G], F32, name="y")
+        y = sb.tile([P, PACK, G], F32, name="y", align_bytes=256)
         for t in range(PACK):
             codes, scales = wo_q[t]
             bank = banks[(2, 3, 5, 6)[t]]
@@ -307,7 +304,7 @@ def tile_attend_filterconv_pl_kernel(tc, rad, wr, atom, wo, offs, out_0, out_1, 
         y_bf = sb.tile([P, G * PACK], BF16, name="y_bf", align_bytes=64)
         y_dst = y_bf[:].rearrange("p (c i t) -> p c t i", i=4, t=PACK)
         y_src = y[:].rearrange("p t (c i) -> p c t i", i=4)
-        y_codes = sb.tile([P, G], U32, name="y_codes", align_bytes=64)
+        y_codes = sb.tile([P, G], U32, name="y_codes", align_bytes=256)
         y_scales = sb.tile([P, G], U8, name="y_scales", align_bytes=64)
         nc.vector.tensor_copy(y_dst[:, :, 0:2, :], y_src[:, :, 0:2, :])
         for h in range(2):

@@ -153,10 +153,16 @@ def tile_attend_filterconv_pl_kernel(tc, rad, wr, atom, wo, offs, out_0, out_1, 
                 x[t][:, lo:hi], picked[t][:, lo - fused[t] : hi - fused[t]], filters(t, lo, hi), MULT
             )
 
+        sums_banks = (banks[0], banks[3])
+
+        def turn_back(t, sums):
+            nc.scalar.copy(sums, sums_banks[t][:, :P])
+            nc.tensor.transpose(banks[1][:, t * G : (t + 1) * G], sums, ident[:])
+
         def tensor_sums(t):
             for e in range(EDGES):
                 nc.tensor.matmul(
-                    banks[0][:, t * P : (t + 1) * P],
+                    sums_banks[t][:, :P],
                     x[t][:, e:I:EDGES],
                     ident[:],
                     start=(e == 0),
@@ -175,19 +181,19 @@ def tile_attend_filterconv_pl_kernel(tc, rad, wr, atom, wo, offs, out_0, out_1, 
                 for q in range(2):
                     empty_filters(t + 1, q * PIECE, (q + 1) * PIECE)
             if t == 2:
-                fourth = sb.tile([P, LAST_FUSED + 3 * P], F32, name="fourth", tag="atom2", align_bytes=256)
+                fourth = sb.tile([P, LAST_FUSED + 4 * P], F32, name="fourth", tag="atom2", align_bytes=256)
                 z.append(fourth[:, :LAST_FUSED])
                 empty_filters(3, 0, LAST_FUSED - LEAD)
-                shared = LAST_FUSED + P
+                shared = LAST_FUSED + 2 * P
                 lead_filters = fourth[:, shared - LEAD // 2 : shared + LEAD // 2]
                 nc.scalar.copy(lead_filters, filters(last, LAST_FUSED - LEAD, LAST_FUSED))
+                turn_back(0, fourth[:, shared - 2 * P : shared - P])
             for q in (2, 3):
                 product(t, q * PIECE, (q + 1) * PIECE)
             if t < 2:
                 tensor_sums(t)
             if t == 1:
                 make_filters(last, HALF, I)
-        sums_pair = fourth[:, shared - P : shared]
         b_bf = fourth[:, shared:].bitcast(BF16).rearrange("p (g t) -> p g t", t=PACK)
 
         def vector_sums(t, first, source, terms):
@@ -217,14 +223,10 @@ def tile_attend_filterconv_pl_kernel(tc, rad, wr, atom, wo, offs, out_0, out_1, 
         cuts = (LAST_FUSED, HALF, HALF + P, I - P, I)
         for lo, hi in zip(cuts[:2], cuts[1:3]):
             pick(last, lo, hi)
-        nc.scalar.copy(
-            sums_pair.bitcast(BF16).rearrange("p (k t) -> p k t", t=2),
-            banks[0][:, : 2 * P].rearrange("p (t k) -> p k t", t=2),
-        )
-        nc.tensor.transpose(banks[1][:, :G], sums_pair, ident[:])
+        turn_back(1, fourth[:, shared - P : shared])
         for lo, hi in zip(cuts[2:], cuts[3:]):
             pick(last, lo, hi)
-        nc.scalar.copy(b_bf[:, :, 0:2], banks[1][:, :G].bitcast(BF16).rearrange("p (g t) -> p g t", t=2))
+        nc.scalar.copy(b_bf[:, :, 0:2], banks[1][:, : 2 * G].rearrange("p (t g) -> p g t", t=2))
         vector_sums(2, 0, halves[:], EDGES // 2)
         product(last, cuts[0], cuts[1])
         product(last, cuts[1], cuts[2])

@@ -134,7 +134,7 @@ def tile_attend_filterconv_pl_kernel(tc, rad, wr, atom, wo, offs, out_0, out_1, 
         fused = [HALF, HALF, HALF, LAST_FUSED]
         x = [sb.tile([P, I], F32, name="x%d" % t)[:] for t in range(PACK)]
         z = [sb.tile([P, HALF], F32, name="z")[:]] * last
-        picked = [x[1], x[2], x[3], x[0]]
+        picked = [sb.tile([P, I - fused[t]], F32, name="picked%d" % t)[:] for t in range(PACK)]
 
         def empty_filters(t, lo, hi):
             nc.scalar.copy(z[t][:, lo:hi], filters(t, lo, hi))
@@ -170,8 +170,8 @@ def tile_attend_filterconv_pl_kernel(tc, rad, wr, atom, wo, offs, out_0, out_1, 
                     is_transpose=True,
                 )
 
-        empty_filters(0, 0, PIECE)
-        nc.vector.tensor_copy(z[0][:, PIECE:HALF], filters(0, PIECE, HALF))
+        for q in range(2):
+            nc.vector.tensor_copy(z[0][:, q * PIECE : (q + 1) * PIECE], filters(0, q * PIECE, (q + 1) * PIECE))
         for t in range(last):
             for q in range(2):
                 fused_product(t, q * PIECE, (q + 1) * PIECE)

@@ -26,7 +26,7 @@ WR_VECTOR = (96, 64)
 RAD_VECTOR = 640
 LAST_FUSED = 256
 LEAD = 64
-WO_VECTOR = 32
+WO_FIRST = 80
 
 
 def tile_attend_filterconv_pl_kernel(tc, rad, wr, atom, wo, offs, out_0, out_1, out_2):
@@ -53,9 +53,9 @@ def tile_attend_filterconv_pl_kernel(tc, rad, wr, atom, wo, offs, out_0, out_1, 
             atoms.append(raw)
         wo_rows = wo.rearrange("(p j) f -> p j f", j=PACK)
         wo_raw = []
-        for h in range(2):
-            raw = sb.tile([P, PACK, F // 2], F32, name="wo_raw%d" % h, tag="wo_raw%d" % h, align_bytes=256)
-            nc.sync.dma_start(raw[:], wo_rows[:, :, h * F // 2 : (h + 1) * F // 2])
+        for h, (lo, hi) in enumerate(((0, PACK * WO_FIRST), (PACK * WO_FIRST, F))):
+            raw = sb.tile([P, PACK, hi - lo], F32, name="wo_raw%d" % h, tag="wo_raw%d" % h, align_bytes=256)
+            nc.sync.dma_start(raw[:], wo_rows[:, :, lo:hi])
             wo_raw.append(raw)
 
         ident = sb.tile([P, P], F32, name="ident")
@@ -241,28 +241,31 @@ def tile_attend_filterconv_pl_kernel(tc, rad, wr, atom, wo, offs, out_0, out_1, 
         wo_first = sb.tile([P, PACK, 64 * PACK], BF16, name="wo_first", align_bytes=64)
         nc.gpsimd.tensor_scalar(
             wo_first[:].rearrange("p t (m j) -> p m t j", j=PACK),
-            wo_raw[0][:].rearrange("p j (m t) -> p m t j", t=PACK),
+            wo_raw[0][:].rearrange("p j (m t) -> p m t j", t=PACK)[:, :64],
             1.0,
             0.0,
             MULT,
             ADD,
         )
-        wo_second = []
-        for u in range(2):
-            pair = sb.tile([P, 2, 64 * PACK], BF16, name="wo_second%d" % u, align_bytes=64)
-            dst = pair[:].rearrange("p t (m j) -> p m j t", j=PACK)
-            src = wo_raw[1][:].rearrange("p j (m t) -> p m j t", t=PACK)[:, :, :, 2 * u : 2 * u + 2]
-            split = WO_VECTOR * u
-            nc.scalar.copy(dst[:, split:], src[:, split:])
-            if split:
-                nc.vector.tensor_copy(dst[:, :split], src[:, :split])
-            wo_second.append(pair)
+        early = WO_FIRST - 64
+        wo_second = [sb.tile([P, 2, 64 * PACK], BF16, name="wo_second%d" % u, align_bytes=64) for u in range(2)]
 
-        early_codes = sb.tile([P, 2, P], U32, name="early_codes", align_bytes=64)
-        late_codes = sb.tile([P, 2, P], U32, name="late_codes", tag="wo_raw1", align_bytes=256)
+        def second_columns(u, h):
+            dst = wo_second[u][:].rearrange("p t (m j) -> p m j t", j=PACK)
+            src = wo_raw[h][:].rearrange("p j (m t) -> p m j t", t=PACK)[:, :, :, 2 * u : 2 * u + 2]
+            return (dst[:, early:], src) if h else (dst[:, :early], src[:, 64:])
+
+        for u in range(2):
+            nc.scalar.copy(*second_columns(u, 0))
+        for u in range(2):
+            dst, src = second_columns(u, 1)
+            nc.scalar.copy(dst, src)
+
+        early_codes = sb.tile([P, last, P], U32, name="early_codes", align_bytes=64)
+        late_codes = sb.tile([P, P], U32, name="late_codes", tag="wo_raw1", align_bytes=256)
         wo_q = []
         for t in range(PACK):
-            codes = (early_codes, late_codes)[t // 2][:, t % 2, :]
+            codes = late_codes[:] if t == last else early_codes[:, t, :]
             scales = sb.tile([P, P], U8, name="wo_scales%d" % t, align_bytes=64)
             wo_q.append((codes, scales))
 
@@ -272,7 +275,7 @@ def tile_attend_filterconv_pl_kernel(tc, rad, wr, atom, wo, offs, out_0, out_1, 
             cols = slice(64 * h, 64 * h + 64)
             nc.vector.quantize_mx(out=codes[:, cols].bitcast(FP8X4), scales=scales[:, cols], in_=source)
 
-        for t in range(2):
+        for t in range(last):
             quantise_wo(t, 0)
         b_codes = sb.tile([P, G], U32, name="b_codes", tag="wo_raw0", align_bytes=256)
         b_scales = sb.tile([P, G], U8, name="b_scales", align_bytes=64)
@@ -281,9 +284,9 @@ def tile_attend_filterconv_pl_kernel(tc, rad, wr, atom, wo, offs, out_0, out_1, 
         )
         for t in range(2):
             quantise_wo(t, 1)
-        for t in range(2, PACK):
-            for h in range(2):
-                quantise_wo(t, h)
+        quantise_wo(2, 1)
+        for h in range(2):
+            quantise_wo(last, h)
         y = sb.tile([P, PACK, G], F32, name="y", align_bytes=256)
         for t in range(PACK):
             codes, scales = wo_q[t]

@@ -279,9 +279,13 @@ def tile_attend_filterconv_pl_kernel(tc, rad, wr, atom, wo, offs, out_0, out_1, 
             quantise_wo(t, 0)
         b_codes = sb.tile([P, G], U32, name="b_codes", tag="wo_raw0", align_bytes=256)
         b_scales = sb.tile([P, G], U8, name="b_scales", align_bytes=64)
-        nc.vector.quantize_mx(
-            out=b_codes[:].bitcast(FP8X4), scales=b_scales[:], in_=b_bf.rearrange("p g t -> p (g t)")
-        )
+        for h in range(2):
+            cols = slice(h * G // 2, (h + 1) * G // 2)
+            nc.vector.quantize_mx(
+                out=b_codes[:, cols].bitcast(FP8X4),
+                scales=b_scales[:, cols],
+                in_=b_bf[:, cols, :].rearrange("p g t -> p (g t)"),
+            )
         for t in range(2):
             quantise_wo(t, 1)
         quantise_wo(2, 1)

@@ -27,6 +27,7 @@ RAD_VECTOR = 640
 LAST_FUSED = 256
 LEAD = 64
 WO_FIRST = 80
+WO_GPSIMD = 68
 
 
 def tile_attend_filterconv_pl_kernel(tc, rad, wr, atom, wo, offs, out_0, out_1, out_2):
@@ -220,7 +221,7 @@ def tile_attend_filterconv_pl_kernel(tc, rad, wr, atom, wo, offs, out_0, out_1, 
         lo, hi = LAST_FUSED - LEAD, LAST_FUSED
         nc.vector.tensor_tensor(x[last][:, lo:hi], window(last, lo, hi), lead_filters, MULT)
         fused_product(last, 0, lo)
-        cuts = (LAST_FUSED, HALF, HALF + P, I - P, I)
+        cuts = (LAST_FUSED, HALF, HALF + 192, I - P, I)
         for lo, hi in zip(cuts[:2], cuts[1:3]):
             pick(last, lo, hi)
         turn_back(1, fourth[:, shared - P : shared])
@@ -233,64 +234,51 @@ def tile_attend_filterconv_pl_kernel(tc, rad, wr, atom, wo, offs, out_0, out_1, 
         piece_sums(last, 0, cuts[0])
         piece_sums(last, cuts[0], cuts[1])
         product(last, cuts[2], cuts[3])
-        piece_sums(last, cuts[1], cuts[2])
         product(last, cuts[3], I)
+        piece_sums(last, cuts[1], cuts[2])
         piece_sums(last, cuts[2], cuts[3])
         piece_sums(last, cuts[3], I)
 
-        wo_first = sb.tile([P, PACK, 64 * PACK], BF16, name="wo_first", align_bytes=64)
+        wo_bf = sb.tile([P, PACK, P * PACK], BF16, name="wo_bf", align_bytes=64)
         nc.gpsimd.tensor_scalar(
-            wo_first[:].rearrange("p t (m j) -> p m t j", j=PACK),
-            wo_raw[0][:].rearrange("p j (m t) -> p m t j", t=PACK)[:, :64],
+            wo_bf[:].rearrange("p t (m j) -> p m t j", j=PACK)[:, :WO_GPSIMD],
+            wo_raw[0][:].rearrange("p j (m t) -> p m t j", t=PACK)[:, :WO_GPSIMD],
             1.0,
             0.0,
             MULT,
             ADD,
         )
-        early = WO_FIRST - 64
-        wo_second = [sb.tile([P, 2, 64 * PACK], BF16, name="wo_second%d" % u, align_bytes=64) for u in range(2)]
-
-        def second_columns(u, h):
-            dst = wo_second[u][:].rearrange("p t (m j) -> p m j t", j=PACK)
-            src = wo_raw[h][:].rearrange("p j (m t) -> p m j t", t=PACK)[:, :, :, 2 * u : 2 * u + 2]
-            return (dst[:, early:], src) if h else (dst[:, :early], src[:, 64:])
-
+        wo_dst = wo_bf[:].rearrange("p t (m j) -> p m j t", j=PACK)
+        wo_src = [raw[:].rearrange("p j (m t) -> p m j t", t=PACK) for raw in wo_raw]
+        nc.scalar.copy(wo_dst[:, WO_GPSIMD:WO_FIRST], wo_src[0][:, WO_GPSIMD:])
         for u in range(2):
-            nc.scalar.copy(*second_columns(u, 0))
-        for u in range(2):
-            dst, src = second_columns(u, 1)
-            nc.scalar.copy(dst, src)
+            nc.scalar.copy(wo_dst[:, WO_FIRST:, :, 2 * u : 2 * u + 2], wo_src[1][:, :, :, 2 * u : 2 * u + 2])
 
-        early_codes = sb.tile([P, last, P], U32, name="early_codes", align_bytes=64)
-        late_codes = sb.tile([P, P], U32, name="late_codes", tag="wo_raw1", align_bytes=256)
         wo_q = []
         for t in range(PACK):
-            codes = late_codes[:] if t == last else early_codes[:, t, :]
+            codes = sb.tile([P, P], U32, name="wo_codes%d" % t, align_bytes=64)
             scales = sb.tile([P, P], U8, name="wo_scales%d" % t, align_bytes=64)
-            wo_q.append((codes, scales))
+            wo_q.append((codes[:], scales))
 
-        def quantise_wo(t, h):
+        def quantise_wo(t, lo, hi):
             codes, scales = wo_q[t]
-            source = wo_second[t // 2][:, t % 2, :] if h else wo_first[:, t, :]
-            cols = slice(64 * h, 64 * h + 64)
-            nc.vector.quantize_mx(out=codes[:, cols].bitcast(FP8X4), scales=scales[:, cols], in_=source)
+            nc.vector.quantize_mx(
+                out=codes[:, lo:hi].bitcast(FP8X4), scales=scales[:, lo:hi], in_=wo_bf[:, t, PACK * lo : PACK * hi]
+            )
 
         for t in range(last):
-            quantise_wo(t, 0)
+            quantise_wo(t, 0, P // 2)
         b_codes = sb.tile([P, G], U32, name="b_codes", tag="wo_raw0", align_bytes=256)
         b_scales = sb.tile([P, G], U8, name="b_scales", align_bytes=64)
-        for h in range(2):
-            cols = slice(h * G // 2, (h + 1) * G // 2)
+        for cols in (slice(0, G // 2), slice(G // 2, G - 32), slice(G - 32, G)):
             nc.vector.quantize_mx(
                 out=b_codes[:, cols].bitcast(FP8X4),
                 scales=b_scales[:, cols],
                 in_=b_bf[:, cols, :].rearrange("p g t -> p (g t)"),
             )
-        for t in range(2):
-            quantise_wo(t, 1)
-        quantise_wo(2, 1)
-        for h in range(2):
-            quantise_wo(last, h)
+        for t in range(last):
+            quantise_wo(t, P // 2, P)
+        quantise_wo(last, 0, P)
         y = sb.tile([P, PACK, G], F32, name="y", align_bytes=256)
         for t in range(PACK):
             codes, scales = wo_q[t]

@@ -270,7 +270,7 @@ def tile_attend_filterconv_pl_kernel(tc, rad, wr, atom, wo, offs, out_0, out_1, 
             quantise_wo(t, 0, P // 2)
         b_codes = sb.tile([P, G], U32, name="b_codes", tag="wo_raw0", align_bytes=256)
         b_scales = sb.tile([P, G], U8, name="b_scales", align_bytes=64)
-        for cols in (slice(0, G // 2), slice(G // 2, G - 32), slice(G - 32, G)):
+        for cols in (slice(0, G // 2), slice(G // 2, G)):
             nc.vector.quantize_mx(
                 out=b_codes[:, cols].bitcast(FP8X4),
                 scales=b_scales[:, cols],

from contextlib import ExitStack

import concourse.mybir as mybir
from concourse.masks import make_identity

R, K, T, I, G, F = 512, 512, 2048, 1024, 128, 512
FLOPS = 2 * R * K * I + 2 * K * F * G

F32 = mybir.dt.float32
BF16 = mybir.dt.bfloat16
I32 = mybir.dt.int32
U32 = mybir.dt.uint32
U16 = mybir.dt.uint16
U8 = mybir.dt.uint8
FP8X4 = mybir.dt.float8_e4m3fn_x4
MULT = mybir.AluOpType.mult
ADD = mybir.AluOpType.add
COPY = mybir.ActivationFunctionType.Copy

P = 128
PACK = 4
EDGES = I // G
HALF = I // 2
PIECE = I // 4
WR_VECTOR = (96, 64)
RAD_VECTOR = 640
LAST_FUSED = 256
LEAD = 64
WO_FIRST = 80
WO_GPSIMD = 68


def tile_attend_filterconv_pl_kernel(tc, rad, wr, atom, wo, offs, out_0, out_1, out_2):
    nc = tc.nc
    with ExitStack() as ctx:
        sb = ctx.enter_context(tc.tile_pool(name="sb", bufs=1))
        ps = ctx.enter_context(tc.psum_pool(name="ps", bufs=1))

        offsets = sb.tile([P, I // 16], U16, name="offsets", align_bytes=256)
        rad_rows = rad.rearrange("(p u e) i -> p u e i", u=2, e=2)
        rad_raw = []
        for u in range(2):
            raw = sb.tile([P, 2, I], F32, name="rad_raw%d" % u, tag="rad_raw%d" % u, align_bytes=256)
            nc.sync.dma_start(raw[:], rad_rows[:, u, :, :])
            rad_raw.append(raw)
        wr_raw = sb.tile([P, PACK, K], F32, name="wr_raw", align_bytes=256)
        nc.sync.dma_start(wr_raw[:], wr.rearrange("(p j) k -> p j k", j=PACK))
        nc.sync.dma_start(offsets[:], offs)
        atom_rows = atom.rearrange("(p t) n -> p t n", t=PACK)
        atoms = []
        for t in range(PACK):
            raw = sb.tile([P, T], F32, name="atom%d" % t, tag="atom%d" % t, align_bytes=256)
            nc.sync.dma_start(raw[:], atom_rows[:, t, :])
            atoms.append(raw)
        wo_rows = wo.rearrange("(p j) f -> p j f", j=PACK)
        wo_raw = []
        for h, (lo, hi) in enumerate(((0, PACK * WO_FIRST), (PACK * WO_FIRST, F))):
            raw = sb.tile([P, PACK, hi - lo], F32, name="wo_raw%d" % h, tag="wo_raw%d" % h, align_bytes=256)
            nc.sync.dma_start(raw[:], wo_rows[:, :, lo:hi])
            wo_raw.append(raw)

        ident = sb.tile([P, P], F32, name="ident")
        make_identity(nc, ident[:])

        banks = [ps.tile([P, HALF], F32, name="bank%d" % n) for n in range(8)]

        rad_bf = [sb.tile([P, HALF * PACK], BF16, name="rad_bf%d" % h, align_bytes=64) for h in range(2)]

        def round_rad(copy, u, lo, hi):
            h = lo // HALF
            dst = rad_bf[h][:].rearrange("p (c i j) -> p c j i", i=4, j=PACK)[:, :, 2 * u : 2 * u + 2, :]
            src = rad_raw[u][:, :, lo:hi].rearrange("p e (c i) -> p c e i", i=4)
            copy(dst[:, (lo - h * HALF) // 4 : (hi - h * HALF) // 4], src)

        for u in range(2):
            round_rad(nc.vector.tensor_copy, u, 0, HALF)
            round_rad(nc.vector.tensor_copy, u, HALF, RAD_VECTOR)
            round_rad(nc.scalar.copy, u, RAD_VECTOR, I)
        rad_codes, rad_scales = [], []
        for h in range(2):
            codes = sb.tile([P, HALF], U32, name="rad_codes%d" % h, align_bytes=64)
            scales = sb.tile([P, HALF], U8, name="rad_scales%d" % h, align_bytes=64)
            nc.vector.quantize_mx(out=codes[:].bitcast(FP8X4), scales=scales[:], in_=rad_bf[h][:])
            rad_codes.append(codes)
            rad_scales.append(scales)

        wr_q = []
        for u in range(2):
            pair = sb.tile([P, 2, P * PACK], BF16, name="wr_bf%d" % u, align_bytes=64)
            dst = pair[:].rearrange("p t (m j) -> p m j t", j=PACK)
            src = wr_raw[:].rearrange("p j (m t) -> p m j t", t=PACK)[:, :, :, 2 * u : 2 * u + 2]
            split = WR_VECTOR[u]
            nc.vector.tensor_copy(dst[:, :split], src[:, :split])
            nc.scalar.copy(dst[:, split:], src[:, split:])
            for e in range(2):
                codes = sb.tile([P, P], U32, name="wr_codes%d" % (2 * u + e), align_bytes=64)
                scales = sb.tile([P, P], U8, name="wr_scales%d" % (2 * u + e), align_bytes=64)
                nc.vector.quantize_mx(out=codes[:].bitcast(FP8X4), scales=scales[:], in_=pair[:, e, :])
                wr_q.append((codes, scales))

        last = PACK - 1
        places = [
            [(0, 0), (1, 0), (2, 0), (2, PIECE)],
            [(3, 0), (3, PIECE), (4, 0), (4, PIECE)],
            [(5, 0), (5, PIECE), (6, 0), (6, PIECE)],
            [(7, 0), (7, PIECE), (4, 0), (4, PIECE)],
        ]

        def filters(t, lo, hi):
            bank, first = places[t][lo // PIECE]
            start = first + lo % PIECE
            return banks[bank][:, start : start + hi - lo]

        def make_filters(t, lo, hi):
            h = lo // HALF
            cols = slice(lo - h * HALF, hi - h * HALF)
            nc.tensor.matmul_mx(
                out=filters(t, lo, hi),
                lhsT=wr_q[t][0][:].bitcast(FP8X4),
                lhsT_scale=wr_q[t][1][:],
                rhs=rad_codes[h][:, cols].bitcast(FP8X4),
                rhs_scale=rad_scales[h][:, cols],
                start=True,
                stop=True,
            )

        make_filters(0, 0, PIECE)
        make_filters(0, PIECE, HALF)
        make_filters(0, HALF, I)
        for t in (1, 2):
            make_filters(t, 0, HALF)
            make_filters(t, HALF, I)
        make_filters(last, 0, HALF)

        fused = [HALF, HALF, HALF, LAST_FUSED]
        x = [sb.tile([P, I], F32, name="x%d" % t)[:] for t in range(PACK)]
        z = [sb.tile([P, HALF], F32, name="z")[:]] * last
        picked = [sb.tile([P, I - fused[t]], F32, name="picked%d" % t)[:] for t in range(PACK)]

        def empty_filters(t, lo, hi):
            nc.scalar.copy(z[t][:, lo:hi], filters(t, lo, hi))

        def window(t, lo, hi):
            return atoms[t][:].indirect(offsets[:, lo // 16 : hi // 16])

        def fused_product(t, lo, hi):
            nc.vector.tensor_tensor(x[t][:, lo:hi], window(t, lo, hi), z[t][:, lo:hi], MULT)

        def pick(t, lo, hi):
            nc.scalar.activation(picked[t][:, lo - fused[t] : hi - fused[t]], window(t, lo, hi), COPY)

        def product(t, lo, hi):
            nc.vector.tensor_tensor(
                x[t][:, lo:hi], picked[t][:, lo - fused[t] : hi - fused[t]], filters(t, lo, hi), MULT
            )

        sums_banks = (banks[0], banks[3])

        def turn_back(t, sums):
            nc.scalar.copy(sums, sums_banks[t][:, :P])
            nc.tensor.transpose(banks[1][:, t * G : (t + 1) * G], sums, ident[:])

        def tensor_sums(t):
            for e in range(EDGES):
                nc.tensor.matmul(
                    sums_banks[t][:, :P],
                    x[t][:, e:I:EDGES],
                    ident[:],
                    start=(e == 0),
                    stop=(e == EDGES - 1),
                    is_transpose=True,
                )

        for q in range(2):
            nc.vector.tensor_copy(z[0][:, q * PIECE : (q + 1) * PIECE], filters(0, q * PIECE, (q + 1) * PIECE))
        for t in range(last):
            for q in range(2):
                fused_product(t, q * PIECE, (q + 1) * PIECE)
            for q in (2, 3):
                pick(t, q * PIECE, (q + 1) * PIECE)
            if t < 2:
                for q in range(2):
                    empty_filters(t + 1, q * PIECE, (q + 1) * PIECE)
            if t == 2:
                fourth = sb.tile([P, LAST_FUSED + 4 * P], F32, name="fourth", tag="atom2", align_bytes=256)
                z.append(fourth[:, :LAST_FUSED])
                empty_filters(3, 0, LAST_FUSED - LEAD)
                shared = LAST_FUSED + 2 * P
                lead_filters = fourth[:, shared - LEAD // 2 : shared + LEAD // 2]
                nc.scalar.copy(lead_filters, filters(last, LAST_FUSED - LEAD, LAST_FUSED))
                turn_back(0, fourth[:, shared - 2 * P : shared - P])
            for q in (2, 3):
                product(t, q * PIECE, (q + 1) * PIECE)
            if t < 2:
                tensor_sums(t)
            if t == 1:
                make_filters(last, HALF, I)
        b_bf = fourth[:, shared:].bitcast(BF16).rearrange("p (g t) -> p g t", t=PACK)

        def vector_sums(t, first, source, terms):
            view = source.rearrange("p (g e) -> p g e", e=terms)
            with nc.allow_low_precision(reason="float32 sum, rounded once to bfloat16 for the quantiser"):
                nc.vector.tensor_reduce(
                    out=b_bf[:, first : first + view.shape[1], t], in_=view, axis=mybir.AxisListType.X, op=ADD
                )

        def piece_sums(t, lo, hi):
            vector_sums(t, lo // EDGES, x[t][:, lo:hi], EDGES)

        halves = sb.tile([P, PIECE], F32, name="halves")
        by_edge = x[2][:, :HALF].rearrange("p (g e) -> p g e", e=EDGES)
        nc.gpsimd.tensor_tensor(
            halves[:].rearrange("p (g e) -> p g e", e=EDGES // 2),
            by_edge[:, :, : EDGES // 2],
            by_edge[:, :, EDGES // 2 :],
            ADD,
        )
        for q in (2, 3):
            piece_sums(2, q * PIECE, (q + 1) * PIECE)

        lo, hi = LAST_FUSED - LEAD, LAST_FUSED
        nc.vector.tensor_tensor(x[last][:, lo:hi], window(last, lo, hi), lead_filters, MULT)
        fused_product(last, 0, lo)
        cuts = (LAST_FUSED, HALF, HALF + 192, I - P, I)
        for lo, hi in zip(cuts[:2], cuts[1:3]):
            pick(last, lo, hi)
        turn_back(1, fourth[:, shared - P : shared])
        for lo, hi in zip(cuts[2:], cuts[3:]):
            pick(last, lo, hi)
        nc.scalar.copy(b_bf[:, :, 0:2], banks[1][:, : 2 * G].rearrange("p (t g) -> p g t", t=2))
        vector_sums(2, 0, halves[:], EDGES // 2)
        product(last, cuts[0], cuts[1])
        product(last, cuts[1], cuts[2])
        piece_sums(last, 0, cuts[0])
        piece_sums(last, cuts[0], cuts[1])
        product(last, cuts[2], cuts[3])
        product(last, cuts[3], I)
        piece_sums(last, cuts[1], cuts[2])
        piece_sums(last, cuts[2], cuts[3])
        piece_sums(last, cuts[3], I)

        wo_bf = sb.tile([P, PACK, P * PACK], BF16, name="wo_bf", align_bytes=64)
        nc.gpsimd.tensor_scalar(
            wo_bf[:].rearrange("p t (m j) -> p m t j", j=PACK)[:, :WO_GPSIMD],
            wo_raw[0][:].rearrange("p j (m t) -> p m t j", t=PACK)[:, :WO_GPSIMD],
            1.0,
            0.0,
            MULT,
            ADD,
        )
        wo_dst = wo_bf[:].rearrange("p t (m j) -> p m j t", j=PACK)
        wo_src = [raw[:].rearrange("p j (m t) -> p m j t", t=PACK) for raw in wo_raw]
        nc.scalar.copy(wo_dst[:, WO_GPSIMD:WO_FIRST], wo_src[0][:, WO_GPSIMD:])
        for u in range(2):
            nc.scalar.copy(wo_dst[:, WO_FIRST:, :, 2 * u : 2 * u + 2], wo_src[1][:, :, :, 2 * u : 2 * u + 2])

        wo_q = []
        for t in range(PACK):
            codes = sb.tile([P, P], U32, name="wo_codes%d" % t, align_bytes=64)
            scales = sb.tile([P, P], U8, name="wo_scales%d" % t, align_bytes=64)
            wo_q.append((codes[:], scales))

        def quantise_wo(t, lo, hi):
            codes, scales = wo_q[t]
            nc.vector.quantize_mx(
                out=codes[:, lo:hi].bitcast(FP8X4), scales=scales[:, lo:hi], in_=wo_bf[:, t, PACK * lo : PACK * hi]
            )

        for t in range(last):
            quantise_wo(t, 0, P // 2)
        b_codes = sb.tile([P, G], U32, name="b_codes", tag="wo_raw0", align_bytes=256)
        b_scales = sb.tile([P, G], U8, name="b_scales", align_bytes=64)
        for cols in (slice(0, G // 2), slice(G // 2, G)):
            nc.vector.quantize_mx(
                out=b_codes[:, cols].bitcast(FP8X4),
                scales=b_scales[:, cols],
                in_=b_bf[:, cols, :].rearrange("p g t -> p (g t)"),
            )
        for t in range(last):
            quantise_wo(t, P // 2, P)
        quantise_wo(last, 0, P)
        y = sb.tile([P, PACK, G], F32, name="y", align_bytes=256)
        for t in range(PACK):
            codes, scales = wo_q[t]
            bank = banks[(2, 3, 5, 6)[t]]
            nc.tensor.matmul_mx(
                out=bank[:, :G],
                lhsT=codes.bitcast(FP8X4),
                lhsT_scale=scales[:],
                rhs=b_codes[:].bitcast(FP8X4),
                rhs_scale=b_scales[:],
                start=True,
                stop=True,
            )
            pieces = 2 if t == last else 1
            for h in range(pieces):
                cols = slice(h * G // pieces, (h + 1) * G // pieces)
                nc.scalar.copy(y[:, t, cols], bank[:, cols])
        nc.sync.dma_start(out_0.rearrange("(p t) g -> p t g", t=PACK), y[:])

        y_bf = sb.tile([P, G * PACK], BF16, name="y_bf", align_bytes=64)
        y_dst = y_bf[:].rearrange("p (c i t) -> p c t i", i=4, t=PACK)
        y_src = y[:].rearrange("p t (c i) -> p c t i", i=4)
        y_codes = sb.tile([P, G], U32, name="y_codes", align_bytes=256)
        y_scales = sb.tile([P, G], U8, name="y_scales", align_bytes=64)
        nc.vector.tensor_copy(y_dst[:, :, 0:2, :], y_src[:, :, 0:2, :])
        for h in range(2):
            groups = slice(h * G // 8, (h + 1) * G // 8)
            nc.vector.tensor_copy(y_dst[:, groups, 2:4, :], y_src[:, groups, 2:4, :])
        for h in range(2):
            cols = slice(h * G // 2, (h + 1) * G // 2)
            nc.vector.quantize_mx(
                out=y_codes[:, cols].bitcast(FP8X4),
                scales=y_scales[:, cols],
                in_=y_bf[:, h * G * PACK // 2 : (h + 1) * G * PACK // 2],
            )
        nc.sync.dma_start(out_1[0].rearrange("l c r -> l (c r)").bitcast(I32), y_codes[:].bitcast(I32))
        scale_rows = out_2[0].bitcast(I32)
        for q in range(4):
            queue = nc.scalar if q % 2 == 0 else nc.sync
            queue.dma_start(scale_rows[4 * q : 4 * q + 4, :], y_scales[32 * q : 32 * q + 4, :].bitcast(I32))
